import numpy as np
import ml_dtypes


def mxq(x, axis, fmt="e4m3"):
    dtype, down = {"e4m3": (ml_dtypes.float8_e4m3fn, 7), "e5m2": (ml_dtypes.float8_e5m2, 14)}[fmt]
    v = np.moveaxis(np.asarray(x, np.float32).astype(ml_dtypes.bfloat16).astype(np.float64), axis, -1)
    blocks = v.reshape(v.shape[:-1] + (-1, 32))
    amax = np.abs(blocks).max(-1, keepdims=True)
    byte = np.maximum(np.where(amax > 0, np.frexp(amax)[1] - 1 + 127, 0) - down, 1)
    scale = np.exp2(byte - 127.0)
    codes = (blocks / scale).astype(np.float32).astype(dtype).astype(np.float64)
    return np.moveaxis((codes * scale).reshape(v.shape), -1, axis)


WIDE = False


def mx_kscale(k):
    if not WIDE:
        return np.ones(k)
    levels = np.array([10, -10, 5, -5, 0])
    if k % 512:
        return np.exp2(np.random.permutation(np.resize(levels, k // 32))).repeat(32)
    a = np.empty((k // 512, 16))
    for p in range(k // 512):
        a[p, :8] = np.random.permutation(np.resize(levels, 8))
        for g in range(8):
            far = levels[np.abs(levels - a[p, g]) >= 10]
            a[p, g + 8] = far[np.random.randint(len(far))]
    return np.exp2(a.ravel()).repeat(32)


def f64(x):
    return np.asarray(x).astype(np.float64)


def striped(idx):
    return np.tile(idx.reshape(-1, 16).T, (8, 1)).astype(np.uint16)


def unstriped(offs):
    return offs[:16].T.reshape(-1).astype(np.int64)


E2M1 = np.array([0.0, 0.5, 1.0, 1.5, 2.0, 3.0, 4.0, 6.0, -0.0, -0.5, -1.0, -1.5, -2.0, -3.0, -4.0, -6.0])


def pack_weight(w, fmt):
    k, n = w.shape
    w = f64(np.asarray(w, np.float32).astype(ml_dtypes.bfloat16)).reshape(k // 32, 32, n)
    amax = np.abs(w).max(1)
    if fmt == "e4m3":
        byte = np.frexp(amax)[1] - 1 + 127 - 7
    else:
        mant, ex = np.frexp(amax / 6.0)
        byte = np.where(mant > 0.5, ex, ex - 1) + 127
    byte = np.clip(np.where(amax > 0, byte, 1), 1, 254)
    scaled = (w * np.exp2(127.0 - byte)[:, None, :]).reshape(k, n).astype(np.float32)
    by_word = np.ascontiguousarray(scaled.reshape(k // 512, 128, 4, n).transpose(0, 1, 3, 2))
    if fmt == "e4m3":
        words = by_word.astype(ml_dtypes.float8_e4m3fn).view(np.uint8)
    else:
        c = by_word.astype(ml_dtypes.float4_e2m1fn).view(np.uint8) & 0xF
        words = (c[..., 0::2] | (c[..., 1::2] << 4)).reshape(k // 512, 128, 2 * n)
    return np.ascontiguousarray(words), np.ascontiguousarray(byte.astype(np.uint8).reshape(k // 512, 16, n))


def unpack_weight(words, scales, fmt):
    g, _, n = scales.shape
    words = np.ascontiguousarray(words).reshape(g, 128, n, -1)
    if fmt == "e4m3":
        vals = words.view(ml_dtypes.float8_e4m3fn).astype(np.float64)
    else:
        nib = np.empty((g, 128, n, 4), np.uint8)
        nib[..., 0::2] = words & 0xF
        nib[..., 1::2] = words >> 4
        vals = E2M1[nib]
    vals = vals * np.repeat(np.exp2(scales.astype(np.float64) - 127.0), 8, axis=1)[..., None]
    return vals.transpose(0, 1, 3, 2).reshape(g * 512, n)


def planes(y):
    n, m = y.shape
    v = y.astype(np.float32).astype(ml_dtypes.bfloat16).astype(np.float64).reshape(n // 32, 32, m)
    top = np.abs(v).max(1)
    byte = np.clip(np.where(top > 0, np.frexp(top)[1] - 1 + 127 - 7, 1), 1, 254)
    codes = (v * np.exp2(127.0 - byte)[:, None, :]).reshape(n, m).astype(np.float32).astype(ml_dtypes.float8_e4m3fn).view(np.uint8)
    words = codes.reshape(n // 512, 128, 4, m).transpose(0, 1, 3, 2)
    return np.ascontiguousarray(words), np.ascontiguousarray(byte.astype(np.uint8).reshape(n // 512, 16, m))


def relu(v):
    return np.maximum(v, 0.0)


K, T, E, C, H, N = 1024, 1024, 6, 128, 512, 512


def by_expert(wq, xq):
    return np.concatenate([wq[e].T @ xq[:, e * C:(e + 1) * C] for e in range(E)], axis=1)


def setup_inputs():
    n = np.random.standard_normal
    s = mx_kscale(K)
    u = mx_kscale(H)
    slot_token = np.random.permutation(T)[:E * C]
    x = pack_weight(n((K, T)) * s[:, None], "e4m3")
    w = [pack_weight(m, "e2m1") for m in n((E, K, N)) / np.sqrt(K) / s[None, :, None]]
    wa = [pack_weight(m, "e4m3") for m in n((E, K, H)) / np.sqrt(K) / s[None, :, None] * u]
    wb = [pack_weight(m, "e4m3") for m in n((E, H, N)) / np.sqrt(H) / u[None, :, None]]
    return {
        "x_words": x[0],
        "x_scales": x[1],
        "w_words": np.stack([m[0] for m in w]),
        "w_scales": np.stack([m[1] for m in w]),
        "wa_words": np.stack([m[0] for m in wa]),
        "wa_scales": np.stack([m[1] for m in wa]),
        "wb_words": np.stack([m[0] for m in wb]),
        "wb_scales": np.stack([m[1] for m in wb]),
        "gate": np.tile(np.random.uniform(0.2, 1.0, E * C), (128, 1)).astype(np.float32),
        "offs": striped(slot_token),
    }


def reference(x_words, x_scales, w_words, w_scales, wa_words, wa_scales, wb_words, wb_scales, gate, offs):
    w = np.stack([unpack_weight(w_words[e], w_scales[e], "e2m1") for e in range(E)])
    wa = np.stack([unpack_weight(wa_words[e], wa_scales[e], "e4m3") for e in range(E)])
    wb = np.stack([unpack_weight(wb_words[e], wb_scales[e], "e4m3") for e in range(E)])
    idx = unstriped(offs)
    xq = unpack_weight(x_words, x_scales, "e4m3")[:, idx]
    h = relu(by_expert(wa, xq))
    y = by_expert(w, xq) + by_expert(wb, mxq(h, 0, "e4m3"))
    out = np.zeros((N, T))
    out[:, idx] = f64(gate[:1]) * y
    out_0 = out
    return (out_0,) + planes(out_0)

@@ -1,0 +1,244 @@
+from contextlib import ExitStack
+
+import concourse.mybir as mybir
+from concourse.masks import make_identity
+
+K, T, E, C, H, N = 1024, 1024, 6, 128, 512, 512
+S = E * C
+FLOPS = 2 * S * (K * H + K * N + H * N)
+
+F32 = mybir.dt.float32
+BF16 = mybir.dt.bfloat16
+I32 = mybir.dt.int32
+U32 = mybir.dt.uint32
+U16 = mybir.dt.uint16
+U8 = mybir.dt.uint8
+FP8X4 = mybir.dt.float8_e4m3fn_x4
+FP4X4 = mybir.dt.float4_e2m1fn_x4
+ACT = mybir.ActivationFunctionType
+
+P = 128
+PASSES = K // 512
+ROW_W, ROW_WA, ROW_WB = 0, 4, 8
+SCALE_GROUPS = ((0, 2), (2, 6))
+GATHER_GROUPS = ((0, 1), (1, 3), (3, 6))
+EARLY_LAST = 2
+HALF = T // 2
+
+
+def tile_moe_elr_relu_kernel(
+    tc, x_words, x_scales, w_words, w_scales, wa_words, wa_scales, wb_words, wb_scales, gate, offs, out_0, out_1, out_2
+):
+    nc = tc.nc
+    with ExitStack() as ctx:
+        keep = ctx.enter_context(tc.tile_pool(name="keep", bufs=1))
+        ring = ctx.enter_context(tc.tile_pool(name="ring", bufs=4))
+        psum = ctx.enter_context(tc.psum_pool(name="psum", bufs=2))
+
+        def held(shape, dtype, name, tag=None):
+            return keep.tile(shape, dtype, name=name, tag=tag or name, align_bytes=64)
+
+        def zero(engine, tile):
+            engine.memset(tile[:].bitcast(I32), 0)
+
+        def load_planes(queues, tile, row, scales, first, last):
+            src = scales[first:last].rearrange("e s (q r) n -> r q (e s) n", r=4)
+            for r in range(4):
+                queues[r * len(queues) // 4].dma_start(tile[row + r : P : 32, :, :].bitcast(I32), src[r].bitcast(I32))
+
+        offsets = held([P, S // 16], U16, "offsets")
+        nc.sync.dma_start(offsets[:], offs)
+        gate_rows = held([P, C], F32, "gate_rows")
+        nc.sync.dma_start(gate_rows[:], gate.rearrange("r (e c) -> (r e) c", c=C)[0:P, :])
+        x_table = held([P, PASSES, T], U32, "x_table")
+        nc.sync.dma_start(x_table[:].bitcast(I32), x_words.rearrange("s p t d -> p s (t d)").bitcast(I32))
+
+        early, late = SCALE_GROUPS
+        x_planes = held([P, T], U8, "x_planes")
+        wa_planes = [held([P, PASSES * (b - a), H], U8, "wa_planes%d" % a) for a, b in SCALE_GROUPS]
+        w_planes = [held([P, PASSES * (b - a), N], U8, "w_planes%d" % a) for a, b in SCALE_GROUPS]
+        wb_planes = held([P, E, N], U8, "wb_planes")
+        second_plane = held([P, S], U8, "second_plane")
+        identity = held([P, P], F32, "identity")
+        zero(nc.gpsimd, x_planes)
+        make_identity(nc, identity[:])
+        zero(nc.gpsimd, wa_planes[0])
+        for tile in (wb_planes, w_planes[0], second_plane, wa_planes[1], w_planes[1]):
+            zero(nc.vector, tile)
+        for q in range(4):
+            nc.scalar.dma_start(
+                x_planes[32 * q : 32 * q + 8, :].bitcast(I32), x_scales[:, 4 * q : 4 * q + 4, :].bitcast(I32)
+            )
+        load_planes((nc.scalar, nc.gpsimd), wa_planes[0], ROW_WA, wa_scales, *early)
+
+        wa_t, w_t, wb_t = {}, {}, {}
+
+        def load_wa(e):
+            wa_t[e] = held([P, PASSES, H], U32, "wa%d" % e)
+            nc.sync.dma_start(wa_t[e][:].bitcast(I32), wa_words[e].rearrange("s p i d -> p s (i d)").bitcast(I32))
+
+        def load_w(e):
+            w_t[e] = held([P, PASSES, 2 * N], U8, "w%d" % e)
+            nc.sync.dma_start(w_t[e][:].bitcast(I32), w_words[e].rearrange("s p b -> p s b").bitcast(I32))
+            wb_t[e] = held([P, N], U32, "wb%d" % e)
+            nc.sync.dma_start(wb_t[e][:].bitcast(I32), wb_words[e, 0].rearrange("p n d -> p (n d)").bitcast(I32))
+
+        load_wa(0)
+        load_wa(1)
+        load_w(0)
+        load_planes((nc.sync,), w_planes[0], ROW_W, w_scales, *early)
+        load_wa(2)
+        load_planes((nc.sync,), wa_planes[1], ROW_WA, wa_scales, *late)
+        load_wa(3)
+        load_w(1)
+        load_wa(4)
+        load_planes((nc.sync,), w_planes[1], ROW_W, w_scales, *late)
+        load_w(2)
+        load_wa(5)
+        for e in range(3, E):
+            load_w(e)
+
+        def weight_plane(kind, e, s):
+            if kind == ROW_WB:
+                return wb_planes[kind:P, e, :]
+            group = 0 if e < late[0] else 1
+            tile = (wa_planes if kind == ROW_WA else w_planes)[group]
+            return tile[kind:P, PASSES * (e - SCALE_GROUPS[group][0]) + s, :]
+
+        load_planes((nc.gpsimd,), wb_planes, ROW_WB, wb_scales, 0, E)
+        gate_bank = psum.tile([P, 4, C], F32, name="gate_bank", tag="yT")
+        nc.tensor.transpose(gate_bank[:, 0, :], gate_rows[:], identity[:])
+        gate_cols = held([P, 8], F32, "gate_cols")
+        nc.scalar.activation(gate_cols[:], gate_bank[:, 0, 0:8], ACT.Copy)
+
+        slot_planes = held([P, S], U8, "slot_planes")
+        nc.vector.tensor_copy(slot_planes[:], x_planes[:].indirect(offsets[:]))
+        nc.gpsimd.dma_start(second_plane[0 : P - 4, :].bitcast(I32), slot_planes[4:P, :].bitcast(I32))
+
+        windows = [held([P, T], F32, "window%d" % t) for t in range(4)]
+        slot_words = {}
+
+        def gather(first, last, tag):
+            tile = held([P, PASSES, (last - first) * C], U32, "slots%d" % first, tag)
+            for s in range(PASSES):
+                nc.vector.tensor_copy(tile[:, s, :], x_table[:, s, :].indirect(offsets[:, 8 * first : 8 * last]))
+            for e in range(first, last):
+                slot_words[e] = [tile[:, s, (e - first) * C : (e - first + 1) * C].bitcast(FP8X4) for s in range(PASSES)]
+
+        gather(*GATHER_GROUPS[0], None)
+        gather(*GATHER_GROUPS[1], None)
+        for t in range(4):
+            (nc.gpsimd if t else nc.vector).memset(windows[t][:], 0.0)
+
+        y_rows = held([P, 4, S], F32, "y_rows")
+
+        def scatter(t, first, last):
+            nc.vector.tensor_copy(windows[t][:].indirect(offsets[:, 8 * first : 8 * last]), y_rows[:, t, first * C : last * C])
+
+        hidden = {}
+
+        def adapter_in(e):
+            slots = slice(e * C, (e + 1) * C)
+            h_bank = psum.tile([P, H], F32, name="h_bank")
+            for s in range(PASSES):
+                nc.tensor.matmul_mx(
+                    h_bank[:], lhsT=slot_words[e][s], lhsT_scale=slot_planes[4 * s : P, slots],
+                    rhs=wa_t[e][:, s, :].bitcast(FP8X4), rhs_scale=weight_plane(ROW_WA, e, s),
+                    start=(s == 0), stop=(s == PASSES - 1),
+                )
+            h_pairs = ring.tile([P, 2, P], F32, name="h_pairs", align_bytes=64)
+            nc.scalar.activation(
+                h_pairs[:].bitcast(BF16).rearrange("c u (p j) -> c u p j", j=2),
+                h_bank[:].rearrange("c (p u j) -> c u p j", u=2, j=2),
+                ACT.Relu,
+            )
+            hT_bank = psum.tile([P, 2, C], F32, name="hT_bank")
+            for u in range(2):
+                nc.tensor.transpose(hT_bank[:, u, :], h_pairs[:, u, :], identity[:])
+            if e == 0:
+                h_grouped = held([P, C, 2], F32, "h_grouped0", "held_back")
+            else:
+                h_grouped = ring.tile([P, C, 2], F32, name="h_grouped", align_bytes=64)
+            nc.scalar.copy(h_grouped[:], hT_bank[:].rearrange("p u c -> p c u"))
+            h_words = ring.tile([P, C], U32, name="h_words", align_bytes=64)
+            h_plane = ring.tile([P, C], U8, name="h_plane", align_bytes=64)
+            nc.vector.quantize_mx(
+                h_words[:].bitcast(FP8X4), h_plane[:], h_grouped[:].rearrange("p c u -> p (c u)").bitcast(BF16)
+            )
+            if e == 0:
+                gather(*GATHER_GROUPS[2], "held_back")
+            hidden[e] = (h_words, h_plane)
+
+        def expert_out(e):
+            slots = slice(e * C, (e + 1) * C)
+            h_words, h_plane = hidden[e]
+            y_bank = psum.tile([P, N], F32, name="y_bank")
+            for s in range(PASSES):
+                nc.tensor.matmul_mx(
+                    y_bank[:], lhsT=slot_words[e][s], lhsT_scale=(slot_planes, second_plane)[s][:, slots],
+                    rhs=w_t[e][:, s, :].bitcast(FP4X4), rhs_scale=weight_plane(ROW_W, e, s),
+                    start=(s == 0), stop=False,
+                )
+            nc.tensor.matmul_mx(
+                y_bank[:], lhsT=h_words[:].bitcast(FP8X4), lhsT_scale=h_plane[:],
+                rhs=wb_t[e][:].bitcast(FP8X4), rhs_scale=weight_plane(ROW_WB, e, 0), start=False, stop=True,
+            )
+            y_dealt = ring.tile([P, 4, P], F32, name="y_dealt", align_bytes=64)
+            nc.scalar.activation(
+                y_dealt[:], y_bank[:].rearrange("c (p t) -> c t p", t=4), ACT.Copy, scale=gate_cols[:, e : e + 1]
+            )
+            yT_bank = psum.tile([P, 4, C], F32, name="yT_bank", tag="yT")
+            for t in range(4):
+                nc.tensor.transpose(yT_bank[:, t, :], y_dealt[:, t, :], identity[:])
+            nc.scalar.copy(y_rows[:, :, slots], yT_bank[:])
+            for t in range(3):
+                scatter(t, e, e + 1)
+            if e == EARLY_LAST - 1:
+                scatter(3, 0, EARLY_LAST)
+
+        adapter_in(0)
+        adapter_in(1)
+        expert_out(0)
+        adapter_in(2)
+        for e in range(1, E):
+            if e + 2 < E:
+                adapter_in(e + 2)
+            expert_out(e)
+        scatter(3, EARLY_LAST, E)
+
+        out_rows = out_0.rearrange("(p t) c -> p t c", t=4)
+        pairs = [held([P, 2, HALF], F32, "pairs%d" % g) for g in range(2)]
+
+        def pair_view(g, u):
+            return pairs[g][:, u, :].bitcast(BF16).rearrange("p (c j) -> p c j", j=2)
+
+        for t in range(4):
+            nc.sync.dma_start(out_rows[:, t, :], windows[t][:])
+            u, j = divmod(t, 2)
+            for g in range(2):
+                cols = windows[t][:, g * HALF : (g + 1) * HALF]
+                if t == 3 and g == 0:
+                    nc.vector.tensor_copy(pair_view(g, u)[:, :, j], cols)
+                elif t == 2 and g == 0:
+                    nc.scalar.copy(pair_view(g, u), cols.unsqueeze(2).to_broadcast([P, HALF, 2]))
+                else:
+                    nc.scalar.copy(pair_view(g, u)[:, :, j], cols)
+
+        out_words = held([P, T], U32, "out_words")
+        out_plane = held([P, T], U8, "out_plane")
+        words_dram = out_1[0].rearrange("p t d -> p (t d)").bitcast(I32)
+        for g in range(2):
+            cols = slice(g * HALF, (g + 1) * HALF)
+            grouped = held([P, HALF, 2], F32, "grouped%d" % g)
+            if g == 0:
+                nc.vector.tensor_copy(grouped[:].bitcast(I32), pairs[g][:].bitcast(I32).rearrange("p u c -> p c u"))
+            else:
+                nc.scalar.copy(grouped[:], pairs[g][:].rearrange("p u c -> p c u"))
+            nc.vector.quantize_mx(
+                out_words[:, cols].bitcast(FP8X4), out_plane[:, cols],
+                grouped[:].rearrange("p c u -> p (c u)").bitcast(BF16),
+            )
+            nc.sync.dma_start(words_dram[:, cols], out_words[:, cols].bitcast(I32))
+        plane_dram = out_2[0].rearrange("(q r) t -> r q t", r=4)
+        for r in range(4):
+            (nc.sync, nc.scalar)[r % 2].dma_start(plane_dram[r].bitcast(I32), out_plane[r:P:32, :].bitcast(I32))

@@ -33,7 +33,7 @@ def tile_moe_elr_relu_kernel(
     with ExitStack() as ctx:
         keep = ctx.enter_context(tc.tile_pool(name="keep", bufs=1))
         ring = ctx.enter_context(tc.tile_pool(name="ring", bufs=4))
-        psum = ctx.enter_context(tc.psum_pool(name="psum", bufs=2))
+        psum = ctx.enter_context(tc.psum_pool(name="psum", bufs=1))
 
         def held(shape, dtype, name, tag=None):
             return keep.tile(shape, dtype, name=name, tag=tag or name, align_bytes=64)
@@ -41,10 +41,18 @@ def tile_moe_elr_relu_kernel(
         def zero(engine, tile):
             engine.memset(tile[:].bitcast(I32), 0)
 
-        def load_planes(queues, tile, row, scales, first, last):
+        def load_planes(queue, tile, row, scales, first, last):
             src = scales[first:last].rearrange("e s (q r) n -> r q (e s) n", r=4)
+            planes = src.shape[2]
             for r in range(4):
-                queues[r * len(queues) // 4].dma_start(tile[row + r : P : 32, :, :].bitcast(I32), src[r].bitcast(I32))
+                queue.dma_start(tile[row + r : P : 32, 0:planes, :].bitcast(I32), src[r].bitcast(I32))
+
+        def load_packed_planes(tile, scales):
+            planes = scales.shape[0]
+            for q in range(4):
+                nc.scalar.dma_start(
+                    tile[32 * q : 32 * q + 4 * planes, :].bitcast(I32), scales[:, 4 * q : 4 * q + 4, :].bitcast(I32)
+                )
 
         offsets = held([P, S // 16], U16, "offsets")
         nc.sync.dma_start(offsets[:], offs)
@@ -55,21 +63,20 @@ def tile_moe_elr_relu_kernel(
 
         early, late = SCALE_GROUPS
         x_planes = held([P, T], U8, "x_planes")
-        wa_planes = [held([P, PASSES * (b - a), H], U8, "wa_planes%d" % a) for a, b in SCALE_GROUPS]
+        wa_early = held([P, H], U8, "wa_early")
+        wa_late = held([P, PASSES * (late[1] - late[0]), H], U8, "wa_late")
         w_planes = [held([P, PASSES * (b - a), N], U8, "w_planes%d" % a) for a, b in SCALE_GROUPS]
-        wb_planes = held([P, E, N], U8, "wb_planes")
         second_plane = held([P, S], U8, "second_plane")
         identity = held([P, P], F32, "identity")
+        windows = [held([P, T], F32, "window%d" % t) for t in range(4)]
         zero(nc.gpsimd, x_planes)
+        zero(nc.gpsimd, wa_early)
         make_identity(nc, identity[:])
-        zero(nc.gpsimd, wa_planes[0])
-        for tile in (wb_planes, w_planes[0], second_plane, wa_planes[1], w_planes[1]):
+        for tile in (w_planes[0], second_plane, wa_late, w_planes[1]):
             zero(nc.vector, tile)
-        for q in range(4):
-            nc.scalar.dma_start(
-                x_planes[32 * q : 32 * q + 8, :].bitcast(I32), x_scales[:, 4 * q : 4 * q + 4, :].bitcast(I32)
-            )
-        load_planes((nc.scalar, nc.gpsimd), wa_planes[0], ROW_WA, wa_scales, *early)
+        load_planes(nc.gpsimd, w_planes[0], ROW_WB, wb_scales, *early)
+        load_packed_planes(x_planes, x_scales)
+        load_packed_planes(wa_early, wa_scales[early[0] : early[1]].rearrange("e s b i -> (e s) b i"))
 
         wa_t, w_t, wb_t = {}, {}, {}
 
@@ -86,27 +93,31 @@ def tile_moe_elr_relu_kernel(
         load_wa(0)
         load_wa(1)
         load_w(0)
-        load_planes((nc.sync,), w_planes[0], ROW_W, w_scales, *early)
+        load_planes(nc.sync, w_planes[0], ROW_W, w_scales, *early)
         load_wa(2)
-        load_planes((nc.sync,), wa_planes[1], ROW_WA, wa_scales, *late)
-        load_wa(3)
+        load_planes(nc.sync, wa_late, ROW_WA, wa_scales, *late)
         load_w(1)
+        load_wa(3)
+        load_planes(nc.sync, w_planes[1], ROW_W, w_scales, *late)
+        load_planes(nc.sync, w_planes[1], ROW_WB, wb_scales, *late)
         load_wa(4)
-        load_planes((nc.sync,), w_planes[1], ROW_W, w_scales, *late)
         load_w(2)
         load_wa(5)
         for e in range(3, E):
             load_w(e)
 
         def weight_plane(kind, e, s):
-            if kind == ROW_WB:
-                return wb_planes[kind:P, e, :]
             group = 0 if e < late[0] else 1
-            tile = (wa_planes if kind == ROW_WA else w_planes)[group]
-            return tile[kind:P, PASSES * (e - SCALE_GROUPS[group][0]) + s, :]
+            i = e - SCALE_GROUPS[group][0]
+            if kind == ROW_WB:
+                return w_planes[group][kind:P, i, :]
+            if kind == ROW_W:
+                return w_planes[group][kind:P, PASSES * i + s, :]
+            if group == 0:
+                return wa_early[4 * (PASSES * i + s) : P, :]
+            return wa_late[kind:P, PASSES * i + s, :]
 
-        load_planes((nc.gpsimd,), wb_planes, ROW_WB, wb_scales, 0, E)
-        gate_bank = psum.tile([P, 4, C], F32, name="gate_bank", tag="yT")
+        gate_bank = psum.tile([P, 4, C], F32, name="gate_bank", tag="bank7")
         nc.tensor.transpose(gate_bank[:, 0, :], gate_rows[:], identity[:])
         gate_cols = held([P, 8], F32, "gate_cols")
         nc.scalar.activation(gate_cols[:], gate_bank[:, 0, 0:8], ACT.Copy)
@@ -114,8 +125,9 @@ def tile_moe_elr_relu_kernel(
         slot_planes = held([P, S], U8, "slot_planes")
         nc.vector.tensor_copy(slot_planes[:], x_planes[:].indirect(offsets[:]))
         nc.gpsimd.dma_start(second_plane[0 : P - 4, :].bitcast(I32), slot_planes[4:P, :].bitcast(I32))
+        for t in range(4):
+            nc.gpsimd.memset(windows[t][:], 0.0)
 
-        windows = [held([P, T], F32, "window%d" % t) for t in range(4)]
         slot_words = {}
 
         def gather(first, last, tag):
@@ -127,8 +139,6 @@ def tile_moe_elr_relu_kernel(
 
         gather(*GATHER_GROUPS[0], None)
         gather(*GATHER_GROUPS[1], None)
-        for t in range(4):
-            (nc.gpsimd if t else nc.vector).memset(windows[t][:], 0.0)
 
         y_rows = held([P, 4, S], F32, "y_rows")
 
@@ -139,7 +149,7 @@ def tile_moe_elr_relu_kernel(
 
         def adapter_in(e):
             slots = slice(e * C, (e + 1) * C)
-            h_bank = psum.tile([P, H], F32, name="h_bank")
+            h_bank = psum.tile([P, H], F32, name="h_bank", tag="bank%d" % (0, 1, 6, 0, 1, 0)[e])
             for s in range(PASSES):
                 nc.tensor.matmul_mx(
                     h_bank[:], lhsT=slot_words[e][s], lhsT_scale=slot_planes[4 * s : P, slots],
@@ -152,7 +162,7 @@ def tile_moe_elr_relu_kernel(
                 h_bank[:].rearrange("c (p u j) -> c u p j", u=2, j=2),
                 ACT.Relu,
             )
-            hT_bank = psum.tile([P, 2, C], F32, name="hT_bank")
+            hT_bank = psum.tile([P, 2, C], F32, name="hT_bank", tag="bank%d" % (2 + e % 2))
             for u in range(2):
                 nc.tensor.transpose(hT_bank[:, u, :], h_pairs[:, u, :], identity[:])
             if e == 0:
@@ -172,7 +182,7 @@ def tile_moe_elr_relu_kernel(
         def expert_out(e):
             slots = slice(e * C, (e + 1) * C)
             h_words, h_plane = hidden[e]
-            y_bank = psum.tile([P, N], F32, name="y_bank")
+            y_bank = psum.tile([P, N], F32, name="y_bank", tag="bank%d" % (4 + e % 2))
             for s in range(PASSES):
                 nc.tensor.matmul_mx(
                     y_bank[:], lhsT=slot_words[e][s], lhsT_scale=(slot_planes, second_plane)[s][:, slots],
@@ -187,7 +197,7 @@ def tile_moe_elr_relu_kernel(
             nc.scalar.activation(
                 y_dealt[:], y_bank[:].rearrange("c (p t) -> c t p", t=4), ACT.Copy, scale=gate_cols[:, e : e + 1]
             )
-            yT_bank = psum.tile([P, 4, C], F32, name="yT_bank", tag="yT")
+            yT_bank = psum.tile([P, 4, C], F32, name="yT_bank", tag="bank%d" % (6 + e % 2))
             for t in range(4):
                 nc.tensor.transpose(yT_bank[:, t, :], y_dealt[:, t, :], identity[:])
             nc.scalar.copy(y_rows[:, :, slots], yT_bank[:])

@@ -21,9 +21,9 @@ P = 128
 PASSES = K // 512
 ROW_W, ROW_WA, ROW_WB = 0, 4, 8
 SCALE_GROUPS = ((0, 2), (2, 6))
-GATHER_GROUPS = ((0, 1), (1, 3), (3, 6))
-EARLY_LAST = 2
+AT_ONCE = (6, 6, 4, 3)
 HALF = T // 2
+QUARTER = T // 4
 
 
 def tile_moe_elr_relu_kernel(
@@ -32,7 +32,6 @@ def tile_moe_elr_relu_kernel(
     nc = tc.nc
     with ExitStack() as ctx:
         keep = ctx.enter_context(tc.tile_pool(name="keep", bufs=1))
-        ring = ctx.enter_context(tc.tile_pool(name="ring", bufs=4))
         psum = ctx.enter_context(tc.psum_pool(name="psum", bufs=1))
 
         def held(shape, dtype, name, tag=None):
@@ -50,33 +49,41 @@ def tile_moe_elr_relu_kernel(
         def load_packed_planes(tile, scales):
             planes = scales.shape[0]
             for q in range(4):
-                nc.scalar.dma_start(
+                nc.sync.dma_start(
                     tile[32 * q : 32 * q + 4 * planes, :].bitcast(I32), scales[:, 4 * q : 4 * q + 4, :].bitcast(I32)
                 )
 
         offsets = held([P, S // 16], U16, "offsets")
         nc.sync.dma_start(offsets[:], offs)
         gate_rows = held([P, C], F32, "gate_rows")
-        nc.sync.dma_start(gate_rows[:], gate.rearrange("r (e c) -> (r e) c", c=C)[0:P, :])
-        x_table = held([P, PASSES, T], U32, "x_table")
-        nc.sync.dma_start(x_table[:].bitcast(I32), x_words.rearrange("s p t d -> p s (t d)").bitcast(I32))
+        x_table = held([P, PASSES * T], U32, "x_table")
+
+
+        def load_x(s):
+            nc.sync.dma_start(x_table[:, s * T : (s + 1) * T].bitcast(I32), x_words[s].rearrange("p t d -> p (t d)").bitcast(I32))
+
+        load_x(0)
 
         early, late = SCALE_GROUPS
-        x_planes = held([P, T], U8, "x_planes")
+        x_planes = held([P, PASSES, T], U8, "x_planes")
         wa_early = held([P, H], U8, "wa_early")
-        wa_late = held([P, PASSES * (late[1] - late[0]), H], U8, "wa_late")
-        w_planes = [held([P, PASSES * (b - a), N], U8, "w_planes%d" % a) for a, b in SCALE_GROUPS]
-        second_plane = held([P, S], U8, "second_plane")
+        early_planes = held([P, PASSES * (early[1] - early[0]), N], U8, "early_planes")
+        wb_planes = held([P, E, N], U8, "wb_planes")
+        late_planes = held([P, PASSES * (late[1] - late[0]), N], U8, "late_planes")
         identity = held([P, P], F32, "identity")
-        windows = [held([P, T], F32, "window%d" % t) for t in range(4)]
-        zero(nc.gpsimd, x_planes)
-        zero(nc.gpsimd, wa_early)
+        windows = {t: held([P, T], F32, "window%d" % t) for t in range(4)}
         make_identity(nc, identity[:])
-        for tile in (w_planes[0], second_plane, wa_late, w_planes[1]):
+        zero(nc.gpsimd, wb_planes)
+        load_planes(nc.gpsimd, wb_planes, ROW_WB, wb_scales, 0, E)
+        for tile in (x_planes, wa_early, early_planes):
             zero(nc.vector, tile)
-        load_planes(nc.gpsimd, w_planes[0], ROW_WB, wb_scales, *early)
-        load_packed_planes(x_planes, x_scales)
-        load_packed_planes(wa_early, wa_scales[early[0] : early[1]].rearrange("e s b i -> (e s) b i"))
+        for t in range(4):
+            nc.gpsimd.memset(windows[t][:], 0.0)
+        zero(nc.vector, late_planes)
+        x_rows = x_scales.rearrange("s (q r) t -> r q s t", r=4)
+        for r in range(4):
+            nc.sync.dma_start(x_planes[r:P:32, :, :].bitcast(I32), x_rows[r].bitcast(I32))
+        load_x(1)
 
         wa_t, w_t, wb_t = {}, {}, {}
 
@@ -91,15 +98,16 @@ def tile_moe_elr_relu_kernel(
             nc.sync.dma_start(wb_t[e][:].bitcast(I32), wb_words[e, 0].rearrange("p n d -> p (n d)").bitcast(I32))
 
         load_wa(0)
-        load_wa(1)
+        load_packed_planes(wa_early, wa_scales[early[0] : early[1]].rearrange("e s b i -> (e s) b i"))
         load_w(0)
-        load_planes(nc.sync, w_planes[0], ROW_W, w_scales, *early)
+        load_wa(1)
+        load_planes(nc.sync, early_planes, ROW_W, w_scales, *early)
+        nc.sync.dma_start(gate_rows[:], gate.rearrange("r (e c) -> (r e) c", c=C)[0:P, :])
         load_wa(2)
-        load_planes(nc.sync, wa_late, ROW_WA, wa_scales, *late)
-        load_w(1)
+        load_planes(nc.sync, late_planes, ROW_WA, wa_scales, *late)
         load_wa(3)
-        load_planes(nc.sync, w_planes[1], ROW_W, w_scales, *late)
-        load_planes(nc.sync, w_planes[1], ROW_WB, wb_scales, *late)
+        load_planes(nc.sync, late_planes, ROW_W, w_scales, *late)
+        load_w(1)
         load_wa(4)
         load_w(2)
         load_wa(5)
@@ -107,38 +115,35 @@ def tile_moe_elr_relu_kernel(
             load_w(e)
 
         def weight_plane(kind, e, s):
-            group = 0 if e < late[0] else 1
-            i = e - SCALE_GROUPS[group][0]
             if kind == ROW_WB:
-                return w_planes[group][kind:P, i, :]
+                return wb_planes[kind:P, e, :]
+            if e >= late[0]:
+                return late_planes[kind:P, PASSES * (e - late[0]) + s, :]
             if kind == ROW_W:
-                return w_planes[group][kind:P, PASSES * i + s, :]
-            if group == 0:
-                return wa_early[4 * (PASSES * i + s) : P, :]
-            return wa_late[kind:P, PASSES * i + s, :]
+                return early_planes[kind:P, PASSES * e + s, :]
+            return wa_early[4 * (PASSES * e + s) : P, :]
 
-        gate_bank = psum.tile([P, 4, C], F32, name="gate_bank", tag="bank7")
-        nc.tensor.transpose(gate_bank[:, 0, :], gate_rows[:], identity[:])
-        gate_cols = held([P, 8], F32, "gate_cols")
-        nc.scalar.activation(gate_cols[:], gate_bank[:, 0, 0:8], ACT.Copy)
 
-        slot_planes = held([P, S], U8, "slot_planes")
-        nc.vector.tensor_copy(slot_planes[:], x_planes[:].indirect(offsets[:]))
-        nc.gpsimd.dma_start(second_plane[0 : P - 4, :].bitcast(I32), slot_planes[4:P, :].bitcast(I32))
-        for t in range(4):
-            nc.gpsimd.memset(windows[t][:], 0.0)
+        slot_words, slot_planes = {}, {}
 
-        slot_words = {}
-
-        def gather(first, last, tag):
-            tile = held([P, PASSES, (last - first) * C], U32, "slots%d" % first, tag)
+        def gather_words(first, last):
+            tile = held([P, PASSES, (last - first) * C], U32, "slot_words%d" % first)
             for s in range(PASSES):
-                nc.vector.tensor_copy(tile[:, s, :], x_table[:, s, :].indirect(offsets[:, 8 * first : 8 * last]))
+                end = (s + 1) * T if first == 0 else PASSES * T
+                nc.vector.tensor_copy(tile[:, s, :], x_table[:, s * T : end].indirect(offsets[:, 8 * first : 8 * last]))
             for e in range(first, last):
                 slot_words[e] = [tile[:, s, (e - first) * C : (e - first + 1) * C].bitcast(FP8X4) for s in range(PASSES)]
 
-        gather(*GATHER_GROUPS[0], None)
-        gather(*GATHER_GROUPS[1], None)
+        def gather_planes(first, last, tag=None):
+            tile = held([P, PASSES, (last - first) * C], U8, "slot_planes%d" % first, tag)
+            for s in range(PASSES):
+                nc.vector.tensor_copy(tile[:, s, :], x_planes[:, s, :].indirect(offsets[:, 8 * first : 8 * last]))
+            for e in range(first, last):
+                slot_planes[e] = [tile[:, s, (e - first) * C : (e - first + 1) * C] for s in range(PASSES)]
+
+        gather_planes(0, 2)
+        gather_words(0, 2)
+        gather_words(2, E)
 
         y_rows = held([P, 4, S], F32, "y_rows")
 
@@ -148,15 +153,14 @@ def tile_moe_elr_relu_kernel(
         hidden = {}
 
         def adapter_in(e):
-            slots = slice(e * C, (e + 1) * C)
-            h_bank = psum.tile([P, H], F32, name="h_bank", tag="bank%d" % (0, 1, 6, 0, 1, 0)[e])
+            h_bank = psum.tile([P, H], F32, name="h_bank", tag="bank%d" % (0, 1, 4, 4, 0, 1)[e])
             for s in range(PASSES):
                 nc.tensor.matmul_mx(
-                    h_bank[:], lhsT=slot_words[e][s], lhsT_scale=slot_planes[4 * s : P, slots],
+                    h_bank[:], lhsT=slot_words[e][s], lhsT_scale=slot_planes[e][s],
                     rhs=wa_t[e][:, s, :].bitcast(FP8X4), rhs_scale=weight_plane(ROW_WA, e, s),
                     start=(s == 0), stop=(s == PASSES - 1),
                 )
-            h_pairs = ring.tile([P, 2, P], F32, name="h_pairs", align_bytes=64)
+            h_pairs = held([P, 2, P], F32, "h_pairs%d" % e)
             nc.scalar.activation(
                 h_pairs[:].bitcast(BF16).rearrange("c u (p j) -> c u p j", j=2),
                 h_bank[:].rearrange("c (p u j) -> c u p j", u=2, j=2),
@@ -165,18 +169,15 @@ def tile_moe_elr_relu_kernel(
             hT_bank = psum.tile([P, 2, C], F32, name="hT_bank", tag="bank%d" % (2 + e % 2))
             for u in range(2):
                 nc.tensor.transpose(hT_bank[:, u, :], h_pairs[:, u, :], identity[:])
-            if e == 0:
-                h_grouped = held([P, C, 2], F32, "h_grouped0", "held_back")
-            else:
-                h_grouped = ring.tile([P, C, 2], F32, name="h_grouped", align_bytes=64)
+            h_grouped = held([P, C, 2], F32, "h_grouped%d" % e)
             nc.scalar.copy(h_grouped[:], hT_bank[:].rearrange("p u c -> p c u"))
-            h_words = ring.tile([P, C], U32, name="h_words", align_bytes=64)
-            h_plane = ring.tile([P, C], U8, name="h_plane", align_bytes=64)
+            h_words = held([P, C], U32, "h_words%d" % e)
+            h_plane = held([P, C], U8, "h_plane%d" % e)
             nc.vector.quantize_mx(
                 h_words[:].bitcast(FP8X4), h_plane[:], h_grouped[:].rearrange("p c u -> p (c u)").bitcast(BF16)
             )
             if e == 0:
-                gather(*GATHER_GROUPS[2], "held_back")
+                gather_planes(2, E, "h_grouped0")
             hidden[e] = (h_words, h_plane)
 
         def expert_out(e):
@@ -185,7 +186,7 @@ def tile_moe_elr_relu_kernel(
             y_bank = psum.tile([P, N], F32, name="y_bank", tag="bank%d" % (4 + e % 2))
             for s in range(PASSES):
                 nc.tensor.matmul_mx(
-                    y_bank[:], lhsT=slot_words[e][s], lhsT_scale=(slot_planes, second_plane)[s][:, slots],
+                    y_bank[:], lhsT=slot_words[e][s], lhsT_scale=slot_planes[e][s],
                     rhs=w_t[e][:, s, :].bitcast(FP4X4), rhs_scale=weight_plane(ROW_W, e, s),
                     start=(s == 0), stop=False,
                 )
@@ -193,20 +194,26 @@ def tile_moe_elr_relu_kernel(
                 y_bank[:], lhsT=h_words[:].bitcast(FP8X4), lhsT_scale=h_plane[:],
                 rhs=wb_t[e][:].bitcast(FP8X4), rhs_scale=weight_plane(ROW_WB, e, 0), start=False, stop=True,
             )
-            y_dealt = ring.tile([P, 4, P], F32, name="y_dealt", align_bytes=64)
-            nc.scalar.activation(
-                y_dealt[:], y_bank[:].rearrange("c (p t) -> c t p", t=4), ACT.Copy, scale=gate_cols[:, e : e + 1]
-            )
-            yT_bank = psum.tile([P, 4, C], F32, name="yT_bank", tag="bank%d" % (6 + e % 2))
+            pieces = ((0, 2, 6), (2, 4, 7)) if e == 0 else ((0, 4, 6 + (e + 1) % 2),)
+            for t0, t1, bank in pieces:
+                y_dealt = held([P, t1 - t0, P], F32, "y_dealt%d_%d" % (e, t0))
+                nc.scalar.activation(
+                    y_dealt[:], y_bank[:].rearrange("c (p t) -> c t p", t=4)[:, t0:t1, :], ACT.Copy,
+                    scale=gate_cols[:, e : e + 1],
+                )
+                yT_bank = psum.tile([P, t1 - t0, C], F32, name="yT_bank", tag="bank%d" % bank)
+                for t in range(t0, t1):
+                    nc.tensor.transpose(yT_bank[:, t - t0, :], y_dealt[:, t - t0, :], identity[:])
+                nc.scalar.copy(y_rows[:, t0:t1, slots], yT_bank[:])
             for t in range(4):
-                nc.tensor.transpose(yT_bank[:, t, :], y_dealt[:, t, :], identity[:])
-            nc.scalar.copy(y_rows[:, :, slots], yT_bank[:])
-            for t in range(3):
-                scatter(t, e, e + 1)
-            if e == EARLY_LAST - 1:
-                scatter(3, 0, EARLY_LAST)
+                if e < AT_ONCE[t]:
+                    scatter(t, e, e + 1)
 
         adapter_in(0)
+        gate_bank = psum.tile([P, 4, C], F32, name="gate_bank", tag="bank7")
+        nc.tensor.transpose(gate_bank[:, 0, :], gate_rows[:], identity[:])
+        gate_cols = held([P, 8], F32, "gate_cols")
+        nc.scalar.activation(gate_cols[:], gate_bank[:, 0, 0:8], ACT.Copy)
         adapter_in(1)
         expert_out(0)
         adapter_in(2)
@@ -214,7 +221,9 @@ def tile_moe_elr_relu_kernel(
             if e + 2 < E:
                 adapter_in(e + 2)
             expert_out(e)
-        scatter(3, EARLY_LAST, E)
+        for t in range(4):
+            if AT_ONCE[t] < E:
+                scatter(t, AT_ONCE[t], E)
 
         out_rows = out_0.rearrange("(p t) c -> p t c", t=4)
         pairs = [held([P, 2, HALF], F32, "pairs%d" % g) for g in range(2)]
@@ -237,18 +246,23 @@ def tile_moe_elr_relu_kernel(
         out_words = held([P, T], U32, "out_words")
         out_plane = held([P, T], U8, "out_plane")
         words_dram = out_1[0].rearrange("p t d -> p (t d)").bitcast(I32)
-        for g in range(2):
-            cols = slice(g * HALF, (g + 1) * HALF)
-            grouped = held([P, HALF, 2], F32, "grouped%d" % g)
+        grouped = [held([P, QUARTER, 2], F32, "grouped%d" % q) for q in range(4)]
+        for q in range(4):
+            g, i = divmod(q, 2)
+            words = pairs[g][:, :, i * QUARTER : (i + 1) * QUARTER]
             if g == 0:
-                nc.vector.tensor_copy(grouped[:].bitcast(I32), pairs[g][:].bitcast(I32).rearrange("p u c -> p c u"))
+                nc.vector.tensor_copy(grouped[q][:].bitcast(I32), words.bitcast(I32).rearrange("p u c -> p c u"))
             else:
-                nc.scalar.copy(grouped[:], pairs[g][:].rearrange("p u c -> p c u"))
+                nc.scalar.copy(grouped[q][:], words.rearrange("p u c -> p c u"))
+        for q in range(4):
+            cols = slice(q * QUARTER, (q + 1) * QUARTER)
             nc.vector.quantize_mx(
                 out_words[:, cols].bitcast(FP8X4), out_plane[:, cols],
-                grouped[:].rearrange("p c u -> p (c u)").bitcast(BF16),
+                grouped[q][:].rearrange("p c u -> p (c u)").bitcast(BF16),
             )
-            nc.sync.dma_start(words_dram[:, cols], out_words[:, cols].bitcast(I32))
+            if q % 2 == 1:
+                done = slice((q - 1) * QUARTER, (q + 1) * QUARTER)
+                nc.sync.dma_start(words_dram[:, done], out_words[:, done].bitcast(I32))
         plane_dram = out_2[0].rearrange("(q r) t -> r q t", r=4)
         for r in range(4):
             (nc.sync, nc.scalar)[r % 2].dma_start(plane_dram[r].bitcast(I32), out_plane[r:P:32, :].bitcast(I32))

@@ -134,14 +134,14 @@ def tile_moe_elr_relu_kernel(
             for e in range(first, last):
                 slot_words[e] = [tile[:, s, (e - first) * C : (e - first + 1) * C].bitcast(FP8X4) for s in range(PASSES)]
 
-        def gather_planes(first, last, tag=None):
-            tile = held([P, PASSES, (last - first) * C], U8, "slot_planes%d" % first, tag)
-            for s in range(PASSES):
-                nc.vector.tensor_copy(tile[:, s, :], x_planes[:, s, :].indirect(offsets[:, 8 * first : 8 * last]))
+        def gather_planes(first, last, s, tag=None):
+            tile = held([P, (last - first) * C], U8, "slot_planes%d_%d" % (first, s), tag)
+            nc.vector.tensor_copy(tile[:], x_planes[:, s, :].indirect(offsets[:, 8 * first : 8 * last]))
             for e in range(first, last):
-                slot_planes[e] = [tile[:, s, (e - first) * C : (e - first + 1) * C] for s in range(PASSES)]
+                slot_planes[e, s] = tile[:, (e - first) * C : (e - first + 1) * C]
 
-        gather_planes(0, 2)
+        for s in range(PASSES):
+            gather_planes(0, 2, s)
         gather_words(0, 2)
         gather_words(2, E)
 
@@ -156,16 +156,17 @@ def tile_moe_elr_relu_kernel(
             h_bank = psum.tile([P, H], F32, name="h_bank", tag="bank%d" % (0, 1, 4, 4, 0, 1)[e])
             for s in range(PASSES):
                 nc.tensor.matmul_mx(
-                    h_bank[:], lhsT=slot_words[e][s], lhsT_scale=slot_planes[e][s],
+                    h_bank[:], lhsT=slot_words[e][s], lhsT_scale=slot_planes[e, s],
                     rhs=wa_t[e][:, s, :].bitcast(FP8X4), rhs_scale=weight_plane(ROW_WA, e, s),
                     start=(s == 0), stop=(s == PASSES - 1),
                 )
+            if e == 0:
+                gather_planes(2, E, 0, "wa0")
             h_pairs = held([P, 2, P], F32, "h_pairs%d" % e)
-            nc.scalar.activation(
-                h_pairs[:].bitcast(BF16).rearrange("c u (p j) -> c u p j", j=2),
-                h_bank[:].rearrange("c (p u j) -> c u p j", u=2, j=2),
-                ACT.Relu,
-            )
+            rounded = h_pairs[:].bitcast(BF16).rearrange("c u (p j) -> c u p j", j=2)
+            sums = h_bank[:].rearrange("c (p u j) -> c u p j", u=2, j=2)
+            for u0, u1 in ((0, 1), (1, 2)) if e == 0 else ((0, 2),):
+                nc.scalar.activation(rounded[:, u0:u1], sums[:, u0:u1], ACT.Relu)
             hT_bank = psum.tile([P, 2, C], F32, name="hT_bank", tag="bank%d" % (2 + e % 2))
             for u in range(2):
                 nc.tensor.transpose(hT_bank[:, u, :], h_pairs[:, u, :], identity[:])
@@ -177,7 +178,7 @@ def tile_moe_elr_relu_kernel(
                 h_words[:].bitcast(FP8X4), h_plane[:], h_grouped[:].rearrange("p c u -> p (c u)").bitcast(BF16)
             )
             if e == 0:
-                gather_planes(2, E, "h_grouped0")
+                gather_planes(2, E, 1, "h_grouped0")
             hidden[e] = (h_words, h_plane)
 
         def expert_out(e):
@@ -186,7 +187,7 @@ def tile_moe_elr_relu_kernel(
             y_bank = psum.tile([P, N], F32, name="y_bank", tag="bank%d" % (4 + e % 2))
             for s in range(PASSES):
                 nc.tensor.matmul_mx(
-                    y_bank[:], lhsT=slot_words[e][s], lhsT_scale=slot_planes[e][s],
+                    y_bank[:], lhsT=slot_words[e][s], lhsT_scale=slot_planes[e, s],
                     rhs=w_t[e][:, s, :].bitcast(FP4X4), rhs_scale=weight_plane(ROW_W, e, s),
                     start=(s == 0), stop=False,
                 )
@@ -194,7 +195,7 @@ def tile_moe_elr_relu_kernel(
                 y_bank[:], lhsT=h_words[:].bitcast(FP8X4), lhsT_scale=h_plane[:],
                 rhs=wb_t[e][:].bitcast(FP8X4), rhs_scale=weight_plane(ROW_WB, e, 0), start=False, stop=True,
             )
-            pieces = ((0, 2, 6), (2, 4, 7)) if e == 0 else ((0, 4, 6 + (e + 1) % 2),)
+            pieces = ((0, 1, 6), (1, 4, 7)) if e == 0 else ((0, 4, 6 + (e + 1) % 2),)
             for t0, t1, bank in pieces:
                 y_dealt = held([P, t1 - t0, P], F32, "y_dealt%d_%d" % (e, t0))
                 nc.scalar.activation(
@@ -236,10 +237,8 @@ def tile_moe_elr_relu_kernel(
             u, j = divmod(t, 2)
             for g in range(2):
                 cols = windows[t][:, g * HALF : (g + 1) * HALF]
-                if t == 3 and g == 0:
+                if u == 1 and g == 0:
                     nc.vector.tensor_copy(pair_view(g, u)[:, :, j], cols)
-                elif t == 2 and g == 0:
-                    nc.scalar.copy(pair_view(g, u), cols.unsqueeze(2).to_broadcast([P, HALF, 2]))
                 else:
                     nc.scalar.copy(pair_view(g, u)[:, :, j], cols)
 

@@ -80,6 +80,8 @@ def tile_moe_elr_relu_kernel(
         for t in range(4):
             nc.gpsimd.memset(windows[t][:], 0.0)
         zero(nc.vector, late_planes)
+        late_w_planes = held([P, PASSES * (late[1] - late[0]), N], U8, "late_w_planes")
+        zero(nc.vector, late_w_planes)
         x_rows = x_scales.rearrange("s (q r) t -> r q s t", r=4)
         for r in range(4):
             nc.sync.dma_start(x_planes[r:P:32, :, :].bitcast(I32), x_rows[r].bitcast(I32))
@@ -105,9 +107,9 @@ def tile_moe_elr_relu_kernel(
         nc.sync.dma_start(gate_rows[:], gate.rearrange("r (e c) -> (r e) c", c=C)[0:P, :])
         load_wa(2)
         load_planes(nc.sync, late_planes, ROW_WA, wa_scales, *late)
-        load_wa(3)
-        load_planes(nc.sync, late_planes, ROW_W, w_scales, *late)
         load_w(1)
+        load_wa(3)
+        load_planes(nc.sync, late_w_planes, ROW_W, w_scales, *late)
         load_wa(4)
         load_w(2)
         load_wa(5)
@@ -118,7 +120,7 @@ def tile_moe_elr_relu_kernel(
             if kind == ROW_WB:
                 return wb_planes[kind:P, e, :]
             if e >= late[0]:
-                return late_planes[kind:P, PASSES * (e - late[0]) + s, :]
+                return (late_w_planes if kind == ROW_W else late_planes)[kind:P, PASSES * (e - late[0]) + s, :]
             if kind == ROW_W:
                 return early_planes[kind:P, PASSES * e + s, :]
             return wa_early[4 * (PASSES * e + s) : P, :]

@@ -46,10 +46,10 @@ def tile_moe_elr_relu_kernel(
             for r in range(4):
                 queue.dma_start(tile[row + r : P : 32, 0:planes, :].bitcast(I32), src[r].bitcast(I32))
 
-        def load_packed_planes(tile, scales):
+        def load_packed_planes(queue, tile, scales):
             planes = scales.shape[0]
             for q in range(4):
-                nc.sync.dma_start(
+                queue.dma_start(
                     tile[32 * q : 32 * q + 4 * planes, :].bitcast(I32), scales[:, 4 * q : 4 * q + 4, :].bitcast(I32)
                 )
 
@@ -68,20 +68,21 @@ def tile_moe_elr_relu_kernel(
         x_planes = held([P, PASSES, T], U8, "x_planes")
         wa_early = held([P, H], U8, "wa_early")
         early_planes = held([P, PASSES * (early[1] - early[0]), N], U8, "early_planes")
-        wb_planes = held([P, E, N], U8, "wb_planes")
+        wb_early = held([P, N], U8, "wb_early")
+        wb_late = held([P, N], U8, "wb_late")
         late_planes = held([P, PASSES * (late[1] - late[0]), N], U8, "late_planes")
         identity = held([P, P], F32, "identity")
         windows = {t: held([P, T], F32, "window%d" % t) for t in range(4)}
+        zero(nc.gpsimd, wb_early)
+        load_packed_planes(nc.gpsimd, wb_early, wb_scales[0:4, 0])
         make_identity(nc, identity[:])
-        zero(nc.gpsimd, wb_planes)
-        load_planes(nc.gpsimd, wb_planes, ROW_WB, wb_scales, 0, E)
-        for tile in (x_planes, wa_early, early_planes):
+        for tile in (x_planes, wa_early, early_planes, wb_late):
             zero(nc.vector, tile)
+        late_w_planes = held([P, PASSES * (late[1] - late[0]), N], U8, "late_w_planes")
+        zero(nc.gpsimd, late_w_planes)
         for t in range(4):
             nc.gpsimd.memset(windows[t][:], 0.0)
         zero(nc.vector, late_planes)
-        late_w_planes = held([P, PASSES * (late[1] - late[0]), N], U8, "late_w_planes")
-        zero(nc.vector, late_w_planes)
         x_rows = x_scales.rearrange("s (q r) t -> r q s t", r=4)
         for r in range(4):
             nc.sync.dma_start(x_planes[r:P:32, :, :].bitcast(I32), x_rows[r].bitcast(I32))
@@ -100,11 +101,11 @@ def tile_moe_elr_relu_kernel(
             nc.sync.dma_start(wb_t[e][:].bitcast(I32), wb_words[e, 0].rearrange("p n d -> p (n d)").bitcast(I32))
 
         load_wa(0)
-        load_packed_planes(wa_early, wa_scales[early[0] : early[1]].rearrange("e s b i -> (e s) b i"))
-        load_w(0)
-        load_wa(1)
-        load_planes(nc.sync, early_planes, ROW_W, w_scales, *early)
+        load_packed_planes(nc.sync, wa_early, wa_scales[early[0] : early[1]].rearrange("e s b i -> (e s) b i"))
         nc.sync.dma_start(gate_rows[:], gate.rearrange("r (e c) -> (r e) c", c=C)[0:P, :])
+        load_wa(1)
+        load_w(0)
+        load_planes(nc.sync, early_planes, ROW_W, w_scales, *early)
         load_wa(2)
         load_planes(nc.sync, late_planes, ROW_WA, wa_scales, *late)
         load_w(1)
@@ -113,12 +114,14 @@ def tile_moe_elr_relu_kernel(
         load_wa(4)
         load_w(2)
         load_wa(5)
-        for e in range(3, E):
-            load_w(e)
+        load_w(3)
+        load_packed_planes(nc.sync, wb_late, wb_scales[4:E, 0])
+        load_w(4)
+        load_w(5)
 
         def weight_plane(kind, e, s):
             if kind == ROW_WB:
-                return wb_planes[kind:P, e, :]
+                return (wb_early if e < 4 else wb_late)[4 * (e % 4) : P, :]
             if e >= late[0]:
                 return (late_w_planes if kind == ROW_W else late_planes)[kind:P, PASSES * (e - late[0]) + s, :]
             if kind == ROW_W:
@@ -136,14 +139,14 @@ def tile_moe_elr_relu_kernel(
             for e in range(first, last):
                 slot_words[e] = [tile[:, s, (e - first) * C : (e - first + 1) * C].bitcast(FP8X4) for s in range(PASSES)]
 
-        def gather_planes(first, last, s, tag=None):
-            tile = held([P, (last - first) * C], U8, "slot_planes%d_%d" % (first, s), tag)
-            nc.vector.tensor_copy(tile[:], x_planes[:, s, :].indirect(offsets[:, 8 * first : 8 * last]))
-            for e in range(first, last):
-                slot_planes[e, s] = tile[:, (e - first) * C : (e - first + 1) * C]
+        def gather_planes(first, last, tag=None):
+            tile = held([P, PASSES, (last - first) * C], U8, "slot_planes%d" % first, tag)
+            for s in range(PASSES):
+                nc.vector.tensor_copy(tile[:, s, :], x_planes[:, s, :].indirect(offsets[:, 8 * first : 8 * last]))
+                for e in range(first, last):
+                    slot_planes[e, s] = tile[:, s, (e - first) * C : (e - first + 1) * C]
 
-        for s in range(PASSES):
-            gather_planes(0, 2, s)
+        gather_planes(0, 2)
         gather_words(0, 2)
         gather_words(2, E)
 
@@ -155,21 +158,19 @@ def tile_moe_elr_relu_kernel(
         hidden = {}
 
         def adapter_in(e):
-            h_bank = psum.tile([P, H], F32, name="h_bank", tag="bank%d" % (0, 1, 4, 4, 0, 1)[e])
+            h_bank = psum.tile([P, H], F32, name="h_bank", tag="bank%d" % (0, 0, 2, 2, 0, 1)[e])
             for s in range(PASSES):
                 nc.tensor.matmul_mx(
                     h_bank[:], lhsT=slot_words[e][s], lhsT_scale=slot_planes[e, s],
                     rhs=wa_t[e][:, s, :].bitcast(FP8X4), rhs_scale=weight_plane(ROW_WA, e, s),
                     start=(s == 0), stop=(s == PASSES - 1),
                 )
-            if e == 0:
-                gather_planes(2, E, 0, "wa0")
             h_pairs = held([P, 2, P], F32, "h_pairs%d" % e)
             rounded = h_pairs[:].bitcast(BF16).rearrange("c u (p j) -> c u p j", j=2)
             sums = h_bank[:].rearrange("c (p u j) -> c u p j", u=2, j=2)
             for u0, u1 in ((0, 1), (1, 2)) if e == 0 else ((0, 2),):
                 nc.scalar.activation(rounded[:, u0:u1], sums[:, u0:u1], ACT.Relu)
-            hT_bank = psum.tile([P, 2, C], F32, name="hT_bank", tag="bank%d" % (2 + e % 2))
+            hT_bank = psum.tile([P, 2, C], F32, name="hT_bank", tag="bank%d" % (2, 3, 4, 3, 4, 3)[e])
             for u in range(2):
                 nc.tensor.transpose(hT_bank[:, u, :], h_pairs[:, u, :], identity[:])
             h_grouped = held([P, C, 2], F32, "h_grouped%d" % e)
@@ -180,13 +181,13 @@ def tile_moe_elr_relu_kernel(
                 h_words[:].bitcast(FP8X4), h_plane[:], h_grouped[:].rearrange("p c u -> p (c u)").bitcast(BF16)
             )
             if e == 0:
-                gather_planes(2, E, 1, "h_grouped0")
+                gather_planes(2, E, "h_grouped0")
             hidden[e] = (h_words, h_plane)
 
         def expert_out(e):
             slots = slice(e * C, (e + 1) * C)
             h_words, h_plane = hidden[e]
-            y_bank = psum.tile([P, N], F32, name="y_bank", tag="bank%d" % (4 + e % 2))
+            y_bank = psum.tile([P, N], F32, name="y_bank", tag="bank%d" % (2, 5)[e % 2])
             for s in range(PASSES):
                 nc.tensor.matmul_mx(
                     y_bank[:], lhsT=slot_words[e][s], lhsT_scale=slot_planes[e, s],

@@ -73,10 +73,10 @@ def tile_moe_elr_relu_kernel(
         late_planes = held([P, PASSES * (late[1] - late[0]), N], U8, "late_planes")
         identity = held([P, P], F32, "identity")
         windows = {t: held([P, T], F32, "window%d" % t) for t in range(4)}
-        zero(nc.gpsimd, wb_early)
-        load_packed_planes(nc.gpsimd, wb_early, wb_scales[0:4, 0])
+        zero(nc.gpsimd, early_planes)
+        load_planes(nc.gpsimd, early_planes, ROW_W, w_scales, *early)
         make_identity(nc, identity[:])
-        for tile in (x_planes, wa_early, early_planes, wb_late):
+        for tile in (x_planes, wa_early, wb_early, wb_late):
             zero(nc.vector, tile)
         late_w_planes = held([P, PASSES * (late[1] - late[0]), N], U8, "late_w_planes")
         zero(nc.gpsimd, late_w_planes)
@@ -105,7 +105,7 @@ def tile_moe_elr_relu_kernel(
         nc.sync.dma_start(gate_rows[:], gate.rearrange("r (e c) -> (r e) c", c=C)[0:P, :])
         load_wa(1)
         load_w(0)
-        load_planes(nc.sync, early_planes, ROW_W, w_scales, *early)
+        load_packed_planes(nc.sync, wb_early, wb_scales[0:4, 0])
         load_wa(2)
         load_planes(nc.sync, late_planes, ROW_WA, wa_scales, *late)
         load_w(1)

@@ -19,11 +19,10 @@ ACT = mybir.ActivationFunctionType
 
 P = 128
 PASSES = K // 512
-ROW_W, ROW_WA, ROW_WB = 0, 4, 8
-SCALE_GROUPS = ((0, 2), (2, 6))
-AT_ONCE = (6, 6, 4, 3)
-HALF = T // 2
-QUARTER = T // 4
+COLS = C // 16
+EARLY = 2
+ROW_WA = 4
+PIECES = ((0, 384), (384, 640), (640, 1024))
 
 
 def tile_moe_elr_relu_kernel(
@@ -37,58 +36,52 @@ def tile_moe_elr_relu_kernel(
         def held(shape, dtype, name, tag=None):
             return keep.tile(shape, dtype, name=name, tag=tag or name, align_bytes=64)
 
+        def bank(shape, name, number):
+            return psum.tile(shape, F32, name=name, tag="bank%d" % number)
+
         def zero(engine, tile):
             engine.memset(tile[:].bitcast(I32), 0)
 
-        def load_planes(queue, tile, row, scales, first, last):
-            src = scales[first:last].rearrange("e s (q r) n -> r q (e s) n", r=4)
-            planes = src.shape[2]
+        def load_side_by_side(queue, tile, row, scales):
+            src = scales.rearrange("e s (q r) n -> r q (e s) n", r=4)
             for r in range(4):
-                queue.dma_start(tile[row + r : P : 32, 0:planes, :].bitcast(I32), src[r].bitcast(I32))
+                queue.dma_start(tile[row + r : P : 32, :, :].bitcast(I32), src[r].bitcast(I32))
 
-        def load_packed_planes(queue, tile, scales):
-            planes = scales.shape[0]
+        def load_stacked(queue, tile, scales):
+            count = scales.shape[0]
             for q in range(4):
                 queue.dma_start(
-                    tile[32 * q : 32 * q + 4 * planes, :].bitcast(I32), scales[:, 4 * q : 4 * q + 4, :].bitcast(I32)
+                    tile[32 * q : 32 * q + 4 * count, :].bitcast(I32), scales[:, 4 * q : 4 * q + 4, :].bitcast(I32)
                 )
 
         offsets = held([P, S // 16], U16, "offsets")
-        nc.sync.dma_start(offsets[:], offs)
-        gate_rows = held([P, C], F32, "gate_rows")
         x_table = held([P, PASSES * T], U32, "x_table")
-
-
-        def load_x(s):
-            nc.sync.dma_start(x_table[:, s * T : (s + 1) * T].bitcast(I32), x_words[s].rearrange("p t d -> p (t d)").bitcast(I32))
-
-        load_x(0)
-
-        early, late = SCALE_GROUPS
-        x_planes = held([P, PASSES, T], U8, "x_planes")
+        x_bytes = held([P, PASSES, T], U8, "x_bytes")
         wa_early = held([P, H], U8, "wa_early")
-        early_planes = held([P, PASSES * (early[1] - early[0]), N], U8, "early_planes")
-        wb_early = held([P, N], U8, "wb_early")
-        wb_late = held([P, N], U8, "wb_late")
-        late_planes = held([P, PASSES * (late[1] - late[0]), N], U8, "late_planes")
+        wa_late = held([P, PASSES * (E - EARLY), H], U8, "wa_late")
+        w_early = held([P, PASSES * EARLY, N], U8, "w_early")
+        w_late = held([P, PASSES * (E - EARLY), N], U8, "w_late")
+        wb_first = held([P, N], U8, "wb_first")
+        wb_last = held([P, N], U8, "wb_last")
         identity = held([P, P], F32, "identity")
-        windows = {t: held([P, T], F32, "window%d" % t) for t in range(4)}
-        zero(nc.gpsimd, early_planes)
-        load_planes(nc.gpsimd, early_planes, ROW_W, w_scales, *early)
+        gate_rows = held([P, C], F32, "gate_rows")
+        windows = [held([P, T], F32, "window%d" % t) for t in range(4)]
+
+        zero(nc.gpsimd, w_early)
+        load_side_by_side(nc.gpsimd, w_early, 0, w_scales[:EARLY])
         make_identity(nc, identity[:])
-        for tile in (x_planes, wa_early, wb_early, wb_late):
+        for tile in (x_bytes, wa_early, wb_first, wb_last, wa_late):
             zero(nc.vector, tile)
-        late_w_planes = held([P, PASSES * (late[1] - late[0]), N], U8, "late_w_planes")
-        zero(nc.gpsimd, late_w_planes)
+        zero(nc.gpsimd, w_late)
         for t in range(4):
             nc.gpsimd.memset(windows[t][:], 0.0)
-        zero(nc.vector, late_planes)
-        x_rows = x_scales.rearrange("s (q r) t -> r q s t", r=4)
-        for r in range(4):
-            nc.sync.dma_start(x_planes[r:P:32, :, :].bitcast(I32), x_rows[r].bitcast(I32))
-        load_x(1)
 
         wa_t, w_t, wb_t = {}, {}, {}
+
+        def load_x(s):
+            nc.sync.dma_start(
+                x_table[:, s * T : (s + 1) * T].bitcast(I32), x_words[s].rearrange("p t d -> p (t d)").bitcast(I32)
+            )
 
         def load_wa(e):
             wa_t[e] = held([P, PASSES, H], U32, "wa%d" % e)
@@ -97,174 +90,191 @@ def tile_moe_elr_relu_kernel(
         def load_w(e):
             w_t[e] = held([P, PASSES, 2 * N], U8, "w%d" % e)
             nc.sync.dma_start(w_t[e][:].bitcast(I32), w_words[e].rearrange("s p b -> p s b").bitcast(I32))
+
+        def load_wb(e):
             wb_t[e] = held([P, N], U32, "wb%d" % e)
             nc.sync.dma_start(wb_t[e][:].bitcast(I32), wb_words[e, 0].rearrange("p n d -> p (n d)").bitcast(I32))
 
+        nc.sync.dma_start(offsets[:], offs)
+        load_x(0)
+        x_rows = x_scales.rearrange("s (q r) t -> r q s t", r=4)
+        for r in range(4):
+            nc.sync.dma_start(x_bytes[r:P:32, :, :].bitcast(I32), x_rows[r].bitcast(I32))
+        load_x(1)
         load_wa(0)
-        load_packed_planes(nc.sync, wa_early, wa_scales[early[0] : early[1]].rearrange("e s b i -> (e s) b i"))
+        load_stacked(nc.sync, wa_early, wa_scales[:EARLY].rearrange("e s b i -> (e s) b i"))
         nc.sync.dma_start(gate_rows[:], gate.rearrange("r (e c) -> (r e) c", c=C)[0:P, :])
-        load_wa(1)
         load_w(0)
-        load_packed_planes(nc.sync, wb_early, wb_scales[0:4, 0])
-        load_wa(2)
-        load_planes(nc.sync, late_planes, ROW_WA, wa_scales, *late)
+        load_wa(1)
+        load_wb(0)
+        load_stacked(nc.sync, wb_first, wb_scales[0:4, 0])
         load_w(1)
-        load_wa(3)
-        load_planes(nc.sync, late_w_planes, ROW_W, w_scales, *late)
-        load_wa(4)
-        load_w(2)
-        load_wa(5)
-        load_w(3)
-        load_packed_planes(nc.sync, wb_late, wb_scales[4:E, 0])
-        load_w(4)
-        load_w(5)
+        load_side_by_side(nc.sync, wa_late, ROW_WA, wa_scales[EARLY:])
+        load_wa(2)
+        load_wb(1)
+        load_side_by_side(nc.sync, w_late, 0, w_scales[EARLY:])
+        for e in range(2, E):
+            load_w(e)
+            if e + 1 < E:
+                load_wa(e + 1)
+            if e == 4:
+                load_stacked(nc.sync, wb_last, wb_scales[4:E, 0])
+            load_wb(e)
 
-        def weight_plane(kind, e, s):
-            if kind == ROW_WB:
-                return (wb_early if e < 4 else wb_late)[4 * (e % 4) : P, :]
-            if e >= late[0]:
-                return (late_w_planes if kind == ROW_W else late_planes)[kind:P, PASSES * (e - late[0]) + s, :]
-            if kind == ROW_W:
-                return early_planes[kind:P, PASSES * e + s, :]
-            return wa_early[4 * (PASSES * e + s) : P, :]
+        def wa_plane(e, s):
+            if e < EARLY:
+                return wa_early[4 * (PASSES * e + s) : P, :]
+            return wa_late[ROW_WA:P, PASSES * (e - EARLY) + s, :]
 
+        def w_plane(e, s):
+            if e < EARLY:
+                return w_early[:, PASSES * e + s, :]
+            return w_late[:, PASSES * (e - EARLY) + s, :]
 
-        slot_words, slot_planes = {}, {}
+        def wb_plane(e):
+            return (wb_first if e < 4 else wb_last)[4 * (e % 4) : P, :]
+
+        slot_words, slot_bytes = {}, {}
 
         def gather_words(first, last):
             tile = held([P, PASSES, (last - first) * C], U32, "slot_words%d" % first)
             for s in range(PASSES):
                 end = (s + 1) * T if first == 0 else PASSES * T
-                nc.vector.tensor_copy(tile[:, s, :], x_table[:, s * T : end].indirect(offsets[:, 8 * first : 8 * last]))
-            for e in range(first, last):
-                slot_words[e] = [tile[:, s, (e - first) * C : (e - first + 1) * C].bitcast(FP8X4) for s in range(PASSES)]
-
-        def gather_planes(first, last, tag=None):
-            tile = held([P, PASSES, (last - first) * C], U8, "slot_planes%d" % first, tag)
-            for s in range(PASSES):
-                nc.vector.tensor_copy(tile[:, s, :], x_planes[:, s, :].indirect(offsets[:, 8 * first : 8 * last]))
+                nc.vector.tensor_copy(
+                    tile[:, s, :], x_table[:, s * T : end].indirect(offsets[:, COLS * first : COLS * last])
+                )
                 for e in range(first, last):
-                    slot_planes[e, s] = tile[:, s, (e - first) * C : (e - first + 1) * C]
+                    slot_words[e, s] = tile[:, s, (e - first) * C : (e - first + 1) * C].bitcast(FP8X4)
 
-        gather_planes(0, 2)
-        gather_words(0, 2)
-        gather_words(2, E)
+        def gather_bytes(first, last, tag=None):
+            tile = held([P, PASSES, (last - first) * C], U8, "slot_bytes%d" % first, tag)
+            for s in range(PASSES):
+                nc.vector.tensor_copy(tile[:, s, :], x_bytes[:, s, :].indirect(offsets[:, COLS * first : COLS * last]))
+                for e in range(first, last):
+                    slot_bytes[e, s] = tile[:, s, (e - first) * C : (e - first + 1) * C]
+
+        gather_bytes(0, EARLY)
+        gather_words(0, EARLY)
+        gather_words(EARLY, E)
 
         y_rows = held([P, 4, S], F32, "y_rows")
 
-        def scatter(t, first, last):
-            nc.vector.tensor_copy(windows[t][:].indirect(offsets[:, 8 * first : 8 * last]), y_rows[:, t, first * C : last * C])
+        def scatter(t, first, last, on_scalar=False):
+            target = windows[t][:].indirect(offsets[:, COLS * first : COLS * last])
+            values = y_rows[:, t, first * C : last * C]
+            if on_scalar:
+                nc.scalar.activation(target, values, ACT.Copy)
+            else:
+                nc.vector.tensor_copy(target, values)
 
-        hidden = {}
+        h_pairs, hidden, y_dealt = {}, {}, {}
 
-        def adapter_in(e):
-            h_bank = psum.tile([P, H], F32, name="h_bank", tag="bank%d" % (0, 0, 2, 2, 0, 1)[e])
+        def adapter_sum(e):
+            h_bank = bank([P, H], "h_bank", (0, 0, 1, 0, 1, 0)[e])
             for s in range(PASSES):
                 nc.tensor.matmul_mx(
-                    h_bank[:], lhsT=slot_words[e][s], lhsT_scale=slot_planes[e, s],
-                    rhs=wa_t[e][:, s, :].bitcast(FP8X4), rhs_scale=weight_plane(ROW_WA, e, s),
+                    h_bank[:], lhsT=slot_words[e, s], lhsT_scale=slot_bytes[e, s],
+                    rhs=wa_t[e][:, s, :].bitcast(FP8X4), rhs_scale=wa_plane(e, s),
                     start=(s == 0), stop=(s == PASSES - 1),
                 )
-            h_pairs = held([P, 2, P], F32, "h_pairs%d" % e)
-            rounded = h_pairs[:].bitcast(BF16).rearrange("c u (p j) -> c u p j", j=2)
+            h_pairs[e] = held([P, 2, P], F32, "h_pairs%d" % e)
+            rounded = h_pairs[e][:].bitcast(BF16).rearrange("c u (p j) -> c u p j", j=2)
             sums = h_bank[:].rearrange("c (p u j) -> c u p j", u=2, j=2)
             for u0, u1 in ((0, 1), (1, 2)) if e == 0 else ((0, 2),):
                 nc.scalar.activation(rounded[:, u0:u1], sums[:, u0:u1], ACT.Relu)
-            hT_bank = psum.tile([P, 2, C], F32, name="hT_bank", tag="bank%d" % (2, 3, 4, 3, 4, 3)[e])
+
+        def adapter_turn(e):
+            turned = bank([P, 2, C], "h_turned", (4, 3, 2, 3, 2, 3)[e])
             for u in range(2):
-                nc.tensor.transpose(hT_bank[:, u, :], h_pairs[:, u, :], identity[:])
+                nc.tensor.transpose(turned[:, u, :], h_pairs[e][:, u, :], identity[:])
             h_grouped = held([P, C, 2], F32, "h_grouped%d" % e)
-            nc.scalar.copy(h_grouped[:], hT_bank[:].rearrange("p u c -> p c u"))
+            nc.scalar.copy(h_grouped[:], turned[:].rearrange("p u c -> p c u"))
             h_words = held([P, C], U32, "h_words%d" % e)
             h_plane = held([P, C], U8, "h_plane%d" % e)
             nc.vector.quantize_mx(
                 h_words[:].bitcast(FP8X4), h_plane[:], h_grouped[:].rearrange("p c u -> p (c u)").bitcast(BF16)
             )
-            if e == 0:
-                gather_planes(2, E, "h_grouped0")
             hidden[e] = (h_words, h_plane)
 
-        def expert_out(e):
-            slots = slice(e * C, (e + 1) * C)
+        def parts(e):
+            return ((0, 1), (1, 4)) if e == 0 else ((0, 2), (2, 4))
+
+        def result_sum(e):
             h_words, h_plane = hidden[e]
-            y_bank = psum.tile([P, N], F32, name="y_bank", tag="bank%d" % (2, 5)[e % 2])
+            y_bank = bank([P, N], "y_bank", 4 + e % 2)
             for s in range(PASSES):
                 nc.tensor.matmul_mx(
-                    y_bank[:], lhsT=slot_words[e][s], lhsT_scale=slot_planes[e, s],
-                    rhs=w_t[e][:, s, :].bitcast(FP4X4), rhs_scale=weight_plane(ROW_W, e, s),
-                    start=(s == 0), stop=False,
+                    y_bank[:], lhsT=slot_words[e, s], lhsT_scale=slot_bytes[e, s],
+                    rhs=w_t[e][:, s, :].bitcast(FP4X4), rhs_scale=w_plane(e, s), start=(s == 0), stop=False,
                 )
             nc.tensor.matmul_mx(
                 y_bank[:], lhsT=h_words[:].bitcast(FP8X4), lhsT_scale=h_plane[:],
-                rhs=wb_t[e][:].bitcast(FP8X4), rhs_scale=weight_plane(ROW_WB, e, 0), start=False, stop=True,
+                rhs=wb_t[e][:].bitcast(FP8X4), rhs_scale=wb_plane(e), start=False, stop=True,
             )
-            pieces = ((0, 1, 6), (1, 4, 7)) if e == 0 else ((0, 4, 6 + (e + 1) % 2),)
-            for t0, t1, bank in pieces:
-                y_dealt = held([P, t1 - t0, P], F32, "y_dealt%d_%d" % (e, t0))
+            for t0, t1 in parts(e):
+                y_dealt[e, t0] = held([P, t1 - t0, P], F32, "y_dealt%d_%d" % (e, t0))
                 nc.scalar.activation(
-                    y_dealt[:], y_bank[:].rearrange("c (p t) -> c t p", t=4)[:, t0:t1, :], ACT.Copy,
+                    y_dealt[e, t0][:], y_bank[:].rearrange("c (p t) -> c t p", t=4)[:, t0:t1, :], ACT.Copy,
                     scale=gate_cols[:, e : e + 1],
                 )
-                yT_bank = psum.tile([P, t1 - t0, C], F32, name="yT_bank", tag="bank%d" % bank)
-                for t in range(t0, t1):
-                    nc.tensor.transpose(yT_bank[:, t - t0, :], y_dealt[:, t - t0, :], identity[:])
-                nc.scalar.copy(y_rows[:, t0:t1, slots], yT_bank[:])
-            for t in range(4):
-                if e < AT_ONCE[t]:
-                    scatter(t, e, e + 1)
 
-        adapter_in(0)
-        gate_bank = psum.tile([P, 4, C], F32, name="gate_bank", tag="bank7")
-        nc.tensor.transpose(gate_bank[:, 0, :], gate_rows[:], identity[:])
-        gate_cols = held([P, 8], F32, "gate_cols")
-        nc.scalar.activation(gate_cols[:], gate_bank[:, 0, 0:8], ACT.Copy)
-        adapter_in(1)
-        expert_out(0)
-        adapter_in(2)
-        for e in range(1, E):
-            if e + 2 < E:
-                adapter_in(e + 2)
-            expert_out(e)
-        for t in range(4):
-            if AT_ONCE[t] < E:
-                scatter(t, AT_ONCE[t], E)
+        def result_turn(e):
+            for t0, t1 in parts(e):
+                number = 6 if t0 == 0 else 7
+                turned = bank([P, t1 - t0, C], "y_turned", number)
+                for t in range(t0, t1):
+                    nc.tensor.transpose(turned[:, t - t0, :], y_dealt[e, t0][:, t - t0, :], identity[:])
+                nc.scalar.copy(y_rows[:, t0:t1, e * C : (e + 1) * C], turned[:])
+            for t in range(4 if e < 2 else 3):
+                scatter(t, e, e + 1)
+
+        adapter_sum(0)
+        adapter_turn(0)
+        gather_bytes(EARLY, 4, "wa0")
+        gather_bytes(4, E, "h_grouped0")
+        gate_bank = bank([P, C], "gate_bank", 7)
+        nc.tensor.transpose(gate_bank[:], gate_rows[:], identity[:])
+        gate_cols = held([P, E], F32, "gate_cols")
+        nc.scalar.activation(gate_cols[:], gate_bank[:, 0:E], ACT.Copy)
+        for e in range(E):
+            if e + 1 < E:
+                adapter_sum(e + 1)
+            result_sum(e)
+            if e + 1 < E:
+                adapter_turn(e + 1)
+            else:
+                scatter(3, e - 1, e, True)
+            result_turn(e)
+        scatter(3, E - 1, E, True)
+        scatter(3, 2, 4, True)
 
         out_rows = out_0.rearrange("(p t) c -> p t c", t=4)
-        pairs = [held([P, 2, HALF], F32, "pairs%d" % g) for g in range(2)]
-
-        def pair_view(g, u):
-            return pairs[g][:, u, :].bitcast(BF16).rearrange("p (c j) -> p c j", j=2)
-
+        pairs = [held([P, 2, b - a], F32, "pairs%d" % a) for a, b in PIECES]
         for t in range(4):
             nc.sync.dma_start(out_rows[:, t, :], windows[t][:])
             u, j = divmod(t, 2)
-            for g in range(2):
-                cols = windows[t][:, g * HALF : (g + 1) * HALF]
-                if u == 1 and g == 0:
-                    nc.vector.tensor_copy(pair_view(g, u)[:, :, j], cols)
+            for g, (a, b) in enumerate(PIECES):
+                halves = pairs[g][:, u, :].bitcast(BF16).rearrange("p (c j) -> p c j", j=2)
+                if g < 2:
+                    nc.vector.tensor_copy(halves[:, :, j], windows[t][:, a:b])
                 else:
-                    nc.scalar.copy(pair_view(g, u)[:, :, j], cols)
+                    nc.scalar.copy(halves[:, :, j], windows[t][:, a:b])
 
         out_words = held([P, T], U32, "out_words")
         out_plane = held([P, T], U8, "out_plane")
         words_dram = out_1[0].rearrange("p t d -> p (t d)").bitcast(I32)
-        grouped = [held([P, QUARTER, 2], F32, "grouped%d" % q) for q in range(4)]
-        for q in range(4):
-            g, i = divmod(q, 2)
-            words = pairs[g][:, :, i * QUARTER : (i + 1) * QUARTER]
-            if g == 0:
-                nc.vector.tensor_copy(grouped[q][:].bitcast(I32), words.bitcast(I32).rearrange("p u c -> p c u"))
+        grouped = [held([P, b - a, 2], F32, "grouped%d" % a) for a, b in PIECES]
+        for g in range(3):
+            if g < 2:
+                nc.vector.tensor_copy(grouped[g][:].bitcast(I32), pairs[g][:].bitcast(I32).rearrange("p u c -> p c u"))
             else:
-                nc.scalar.copy(grouped[q][:], words.rearrange("p u c -> p c u"))
-        for q in range(4):
-            cols = slice(q * QUARTER, (q + 1) * QUARTER)
+                nc.scalar.copy(grouped[g][:], pairs[g][:].rearrange("p u c -> p c u"))
+        for g, (a, b) in enumerate(PIECES):
             nc.vector.quantize_mx(
-                out_words[:, cols].bitcast(FP8X4), out_plane[:, cols],
-                grouped[q][:].rearrange("p c u -> p (c u)").bitcast(BF16),
+                out_words[:, a:b].bitcast(FP8X4), out_plane[:, a:b],
+                grouped[g][:].rearrange("p c u -> p (c u)").bitcast(BF16),
             )
-            if q % 2 == 1:
-                done = slice((q - 1) * QUARTER, (q + 1) * QUARTER)
-                nc.sync.dma_start(words_dram[:, done], out_words[:, done].bitcast(I32))
+            nc.sync.dma_start(words_dram[:, a:b], out_words[:, a:b].bitcast(I32))
         plane_dram = out_2[0].rearrange("(q r) t -> r q t", r=4)
         for r in range(4):
             (nc.sync, nc.scalar)[r % 2].dma_start(plane_dram[r].bitcast(I32), out_plane[r:P:32, :].bitcast(I32))

@@ -22,7 +22,7 @@ PASSES = K // 512
 COLS = C // 16
 EARLY = 2
 ROW_WA = 4
-PIECES = ((0, 384), (384, 640), (640, 1024))
+PIECE = T // 4
 
 
 def tile_moe_elr_relu_kernel(
@@ -83,17 +83,26 @@ def tile_moe_elr_relu_kernel(
                 x_table[:, s * T : (s + 1) * T].bitcast(I32), x_words[s].rearrange("p t d -> p (t d)").bitcast(I32)
             )
 
-        def load_wa(e):
-            wa_t[e] = held([P, PASSES, H], U32, "wa%d" % e)
-            nc.sync.dma_start(wa_t[e][:].bitcast(I32), wa_words[e].rearrange("s p i d -> p s (i d)").bitcast(I32))
+        def load_wa(first, count=1):
+            tile = held([P, count * PASSES, H], U32, "wa%d" % first)
+            src = wa_words[first : first + count].rearrange("e s p i d -> p (e s) (i d)")
+            nc.sync.dma_start(tile[:].bitcast(I32), src.bitcast(I32))
+            for e in range(count):
+                wa_t[first + e] = tile[:, PASSES * e : PASSES * (e + 1), :]
 
-        def load_w(e):
-            w_t[e] = held([P, PASSES, 2 * N], U8, "w%d" % e)
-            nc.sync.dma_start(w_t[e][:].bitcast(I32), w_words[e].rearrange("s p b -> p s b").bitcast(I32))
+        def load_w(first, count=1):
+            tile = held([P, count * PASSES, 2 * N], U8, "w%d" % first)
+            src = w_words[first : first + count].rearrange("e s p b -> p (e s) b")
+            nc.sync.dma_start(tile[:].bitcast(I32), src.bitcast(I32))
+            for e in range(count):
+                w_t[first + e] = tile[:, PASSES * e : PASSES * (e + 1), :]
 
-        def load_wb(e):
-            wb_t[e] = held([P, N], U32, "wb%d" % e)
-            nc.sync.dma_start(wb_t[e][:].bitcast(I32), wb_words[e, 0].rearrange("p n d -> p (n d)").bitcast(I32))
+        def load_wb(first, count=1):
+            tile = held([P, count, N], U32, "wb%d" % first)
+            src = wb_words[:, 0].rearrange("e p n d -> p e (n d)").bitcast(I32)
+            nc.sync.dma_start(tile[:].bitcast(I32), src[:, first : first + count, :])
+            for e in range(count):
+                wb_t[first + e] = tile[:, e, :]
 
         nc.sync.dma_start(offsets[:], offs)
         load_x(0)
@@ -110,16 +119,17 @@ def tile_moe_elr_relu_kernel(
         load_stacked(nc.sync, wb_first, wb_scales[0:4, 0])
         load_w(1)
         load_side_by_side(nc.sync, wa_late, ROW_WA, wa_scales[EARLY:])
-        load_wa(2)
+        load_wa(2, 2)
         load_wb(1)
         load_side_by_side(nc.sync, w_late, 0, w_scales[EARLY:])
-        for e in range(2, E):
-            load_w(e)
-            if e + 1 < E:
-                load_wa(e + 1)
-            if e == 4:
-                load_stacked(nc.sync, wb_last, wb_scales[4:E, 0])
-            load_wb(e)
+        load_w(2)
+        load_wa(4, 2)
+        load_wb(2)
+        load_w(3)
+        load_wb(3)
+        load_w(4, 2)
+        load_stacked(nc.sync, wb_last, wb_scales[4:E, 0])
+        load_wb(4, 2)
 
         def wa_plane(e, s):
             if e < EARLY:
@@ -201,7 +211,7 @@ def tile_moe_elr_relu_kernel(
 
         def result_sum(e):
             h_words, h_plane = hidden[e]
-            y_bank = bank([P, N], "y_bank", 4 + e % 2)
+            y_bank = bank([P, N], "y_bank", (4, 5, 4, 5, 4, 1)[e])
             for s in range(PASSES):
                 nc.tensor.matmul_mx(
                     y_bank[:], lhsT=slot_words[e, s], lhsT_scale=slot_bytes[e, s],
@@ -209,7 +219,7 @@ def tile_moe_elr_relu_kernel(
                 )
             nc.tensor.matmul_mx(
                 y_bank[:], lhsT=h_words[:].bitcast(FP8X4), lhsT_scale=h_plane[:],
-                rhs=wb_t[e][:].bitcast(FP8X4), rhs_scale=wb_plane(e), start=False, stop=True,
+                rhs=wb_t[e].bitcast(FP8X4), rhs_scale=wb_plane(e), start=False, stop=True,
             )
             for t0, t1 in parts(e):
                 y_dealt[e, t0] = held([P, t1 - t0, P], F32, "y_dealt%d_%d" % (e, t0))
@@ -220,12 +230,12 @@ def tile_moe_elr_relu_kernel(
 
         def result_turn(e):
             for t0, t1 in parts(e):
-                number = 6 if t0 == 0 else 7
+                number = (6 if e < 5 else 2) + (t0 > 0)
                 turned = bank([P, t1 - t0, C], "y_turned", number)
                 for t in range(t0, t1):
                     nc.tensor.transpose(turned[:, t - t0, :], y_dealt[e, t0][:, t - t0, :], identity[:])
                 nc.scalar.copy(y_rows[:, t0:t1, e * C : (e + 1) * C], turned[:])
-            for t in range(4 if e < 2 else 3):
+            for t in range(4 if e < 2 else 2):
                 scatter(t, e, e + 1)
 
         adapter_sum(0)
@@ -237,44 +247,58 @@ def tile_moe_elr_relu_kernel(
         gate_cols = held([P, E], F32, "gate_cols")
         nc.scalar.activation(gate_cols[:], gate_bank[:, 0:E], ACT.Copy)
         for e in range(E):
-            if e + 1 < E:
-                adapter_sum(e + 1)
+            adapters = ((1,), (2, 3), (4, 5), (), (), ())[e]
+            for later in adapters:
+                adapter_sum(later)
             result_sum(e)
-            if e + 1 < E:
-                adapter_turn(e + 1)
-            else:
-                scatter(3, e - 1, e, True)
+            for later in adapters:
+                adapter_turn(later)
             result_turn(e)
-        scatter(3, E - 1, E, True)
+        scatter(2, 4, E, True)
+        scatter(3, 4, E, True)
         scatter(3, 2, 4, True)
+        scatter(2, 2, 4)
 
         out_rows = out_0.rearrange("(p t) c -> p t c", t=4)
-        pairs = [held([P, 2, b - a], F32, "pairs%d" % a) for a, b in PIECES]
         for t in range(4):
             nc.sync.dma_start(out_rows[:, t, :], windows[t][:])
+
+        pairs = [held([P, 2, PIECE], F32, "pairs%d" % g) for g in range(4)]
+
+        def round_rows(t, g, on_scalar=False):
             u, j = divmod(t, 2)
-            for g, (a, b) in enumerate(PIECES):
-                halves = pairs[g][:, u, :].bitcast(BF16).rearrange("p (c j) -> p c j", j=2)
-                if g < 2:
-                    nc.vector.tensor_copy(halves[:, :, j], windows[t][:, a:b])
-                else:
-                    nc.scalar.copy(halves[:, :, j], windows[t][:, a:b])
+            target = pairs[g][:, u, :].bitcast(BF16).rearrange("p (c j) -> p c j", j=2)[:, :, j]
+            values = windows[t][:, g * PIECE : (g + 1) * PIECE]
+            if on_scalar:
+                nc.scalar.copy(target, values)
+            else:
+                nc.vector.tensor_copy(target, values)
+
+        for t in (0, 1):
+            for g in (2, 3, 0, 1):
+                round_rows(t, g)
+        for t in (2, 3):
+            for g in range(4):
+                round_rows(t, g, g >= 2)
 
         out_words = held([P, T], U32, "out_words")
         out_plane = held([P, T], U8, "out_plane")
         words_dram = out_1[0].rearrange("p t d -> p (t d)").bitcast(I32)
-        grouped = [held([P, b - a, 2], F32, "grouped%d" % a) for a, b in PIECES]
-        for g in range(3):
+        grouped = [held([P, PIECE, 2], F32, "grouped%d" % g) for g in range(4)]
+        for g in range(4):
             if g < 2:
                 nc.vector.tensor_copy(grouped[g][:].bitcast(I32), pairs[g][:].bitcast(I32).rearrange("p u c -> p c u"))
             else:
                 nc.scalar.copy(grouped[g][:], pairs[g][:].rearrange("p u c -> p c u"))
-        for g, (a, b) in enumerate(PIECES):
+        for g in range(4):
+            columns = slice(g * PIECE, (g + 1) * PIECE)
             nc.vector.quantize_mx(
-                out_words[:, a:b].bitcast(FP8X4), out_plane[:, a:b],
+                out_words[:, columns].bitcast(FP8X4), out_plane[:, columns],
                 grouped[g][:].rearrange("p c u -> p (c u)").bitcast(BF16),
             )
-            nc.sync.dma_start(words_dram[:, a:b], out_words[:, a:b].bitcast(I32))
+            if g % 2:
+                stored = slice((g - 1) * PIECE, (g + 1) * PIECE)
+                nc.sync.dma_start(words_dram[:, stored], out_words[:, stored].bitcast(I32))
         plane_dram = out_2[0].rearrange("(q r) t -> r q t", r=4)
         for r in range(4):
             (nc.sync, nc.scalar)[r % 2].dma_start(plane_dram[r].bitcast(I32), out_plane[r:P:32, :].bitcast(I32))

@@ -21,7 +21,6 @@ P = 128
 PASSES = K // 512
 COLS = C // 16
 EARLY = 2
-ROW_WA = 4
 PIECE = T // 4
 
 
@@ -42,10 +41,10 @@ def tile_moe_elr_relu_kernel(
         def zero(engine, tile):
             engine.memset(tile[:].bitcast(I32), 0)
 
-        def load_side_by_side(queue, tile, row, scales):
+        def load_side_by_side(queue, tile, scales):
             src = scales.rearrange("e s (q r) n -> r q (e s) n", r=4)
             for r in range(4):
-                queue.dma_start(tile[row + r : P : 32, :, :].bitcast(I32), src[r].bitcast(I32))
+                queue.dma_start(tile[r:P:32, :, :].bitcast(I32), src[r].bitcast(I32))
 
         def load_stacked(queue, tile, scales):
             count = scales.shape[0]
@@ -57,24 +56,25 @@ def tile_moe_elr_relu_kernel(
         offsets = held([P, S // 16], U16, "offsets")
         x_table = held([P, PASSES * T], U32, "x_table")
         x_bytes = held([P, PASSES, T], U8, "x_bytes")
-        wa_early = held([P, H], U8, "wa_early")
-        wa_late = held([P, PASSES * (E - EARLY), H], U8, "wa_late")
-        w_early = held([P, PASSES * EARLY, N], U8, "w_early")
-        w_late = held([P, PASSES * (E - EARLY), N], U8, "w_late")
+        wa_rows = [held([P, H], U8, "wa_rows%d" % pair) for pair in range(E // 2)]
+        w_rows = [held([P, 2 * PASSES, N], U8, "w_rows%d" % pair) for pair in range(E // 2)]
         wb_first = held([P, N], U8, "wb_first")
         wb_last = held([P, N], U8, "wb_last")
         identity = held([P, P], F32, "identity")
         gate_rows = held([P, C], F32, "gate_rows")
         windows = [held([P, T], F32, "window%d" % t) for t in range(4)]
 
-        zero(nc.gpsimd, w_early)
-        load_side_by_side(nc.gpsimd, w_early, 0, w_scales[:EARLY])
+        zero(nc.gpsimd, w_rows[0])
+        load_side_by_side(nc.gpsimd, w_rows[0], w_scales[0:2])
         make_identity(nc, identity[:])
-        for tile in (x_bytes, wa_early, wb_first, wb_last, wa_late):
+        for tile in (x_bytes, wa_rows[0], wb_first, wa_rows[1], wa_rows[2]):
             zero(nc.vector, tile)
-        zero(nc.gpsimd, w_late)
+        zero(nc.gpsimd, w_rows[1])
+        zero(nc.gpsimd, w_rows[2])
         for t in range(4):
             nc.gpsimd.memset(windows[t][:], 0.0)
+        zero(nc.gpsimd, wb_last)
+        load_stacked(nc.gpsimd, wb_last, wb_scales[4:E, 0])
 
         wa_t, w_t, wb_t = {}, {}, {}
 
@@ -111,35 +111,37 @@ def tile_moe_elr_relu_kernel(
             nc.sync.dma_start(x_bytes[r:P:32, :, :].bitcast(I32), x_rows[r].bitcast(I32))
         load_x(1)
         load_wa(0)
-        load_stacked(nc.sync, wa_early, wa_scales[:EARLY].rearrange("e s b i -> (e s) b i"))
+        def load_wa_rows(pair):
+            load_stacked(nc.sync, wa_rows[pair], wa_scales[2 * pair : 2 * pair + 2].rearrange("e s b i -> (e s) b i"))
+
+        load_wa_rows(0)
         nc.sync.dma_start(gate_rows[:], gate.rearrange("r (e c) -> (r e) c", c=C)[0:P, :])
         load_w(0)
         load_wa(1)
         load_wb(0)
         load_stacked(nc.sync, wb_first, wb_scales[0:4, 0])
         load_w(1)
-        load_side_by_side(nc.sync, wa_late, ROW_WA, wa_scales[EARLY:])
         load_wa(2, 2)
+        load_wa_rows(1)
         load_wb(1)
-        load_side_by_side(nc.sync, w_late, 0, w_scales[EARLY:])
         load_w(2)
-        load_wa(4, 2)
+        load_side_by_side(nc.sync, w_rows[1], w_scales[2:4])
+        load_wa(4)
+        load_wa_rows(2)
         load_wb(2)
         load_w(3)
+        load_wa(5)
         load_wb(3)
         load_w(4, 2)
-        load_stacked(nc.sync, wb_last, wb_scales[4:E, 0])
-        load_wb(4, 2)
+        load_side_by_side(nc.sync, w_rows[2], w_scales[4:6])
+        load_wb(4)
+        load_wb(5)
 
         def wa_plane(e, s):
-            if e < EARLY:
-                return wa_early[4 * (PASSES * e + s) : P, :]
-            return wa_late[ROW_WA:P, PASSES * (e - EARLY) + s, :]
+            return wa_rows[e // 2][4 * (PASSES * (e % 2) + s) : P, :]
 
         def w_plane(e, s):
-            if e < EARLY:
-                return w_early[:, PASSES * e + s, :]
-            return w_late[:, PASSES * (e - EARLY) + s, :]
+            return w_rows[e // 2][:, PASSES * (e % 2) + s, :]
 
         def wb_plane(e):
             return (wb_first if e < 4 else wb_last)[4 * (e % 4) : P, :]
@@ -235,8 +237,8 @@ def tile_moe_elr_relu_kernel(
                 for t in range(t0, t1):
                     nc.tensor.transpose(turned[:, t - t0, :], y_dealt[e, t0][:, t - t0, :], identity[:])
                 nc.scalar.copy(y_rows[:, t0:t1, e * C : (e + 1) * C], turned[:])
-            for t in range(4 if e < 2 else 2):
-                scatter(t, e, e + 1)
+            for t in range((4, 4, 3, 4, 2, 2)[e]):
+                scatter(t, e, e + 1, t == 3 and e >= 2)
 
         adapter_sum(0)
         adapter_turn(0)
@@ -247,20 +249,19 @@ def tile_moe_elr_relu_kernel(
         gate_cols = held([P, E], F32, "gate_cols")
         nc.scalar.activation(gate_cols[:], gate_bank[:, 0:E], ACT.Copy)
         for e in range(E):
-            adapters = ((1,), (2, 3), (4, 5), (), (), ())[e]
+            adapters = ((1,), (2, 3), (4,), (5,), (), ())[e]
             for later in adapters:
                 adapter_sum(later)
             result_sum(e)
             for later in adapters:
                 adapter_turn(later)
             result_turn(e)
-        scatter(2, 4, E, True)
         scatter(3, 4, E, True)
-        scatter(3, 2, 4, True)
-        scatter(2, 2, 4)
+        scatter(2, 4, E, True)
+        scatter(3, 2, 3)
 
         out_rows = out_0.rearrange("(p t) c -> p t c", t=4)
-        for t in range(4):
+        for t in (0, 3, 1, 2):
             nc.sync.dma_start(out_rows[:, t, :], windows[t][:])
 
         pairs = [held([P, 2, PIECE], F32, "pairs%d" % g) for g in range(4)]
@@ -277,7 +278,7 @@ def tile_moe_elr_relu_kernel(
         for t in (0, 1):
             for g in (2, 3, 0, 1):
                 round_rows(t, g)
-        for t in (2, 3):
+        for t in (3, 2):
             for g in range(4):
                 round_rows(t, g, g >= 2)
 

@@ -121,16 +121,16 @@ def tile_moe_elr_relu_kernel(
         load_wb(0)
         load_stacked(nc.sync, wb_first, wb_scales[0:4, 0])
         load_w(1)
-        load_wa(2, 2)
+        load_wa(2)
         load_wa_rows(1)
         load_wb(1)
         load_w(2)
         load_side_by_side(nc.sync, w_rows[1], w_scales[2:4])
-        load_wa(4)
-        load_wa_rows(2)
+        load_wa(3)
         load_wb(2)
         load_w(3)
-        load_wa(5)
+        load_wa(4, 2)
+        load_wa_rows(2)
         load_wb(3)
         load_w(4, 2)
         load_side_by_side(nc.sync, w_rows[2], w_scales[4:6])
@@ -237,7 +237,7 @@ def tile_moe_elr_relu_kernel(
                 for t in range(t0, t1):
                     nc.tensor.transpose(turned[:, t - t0, :], y_dealt[e, t0][:, t - t0, :], identity[:])
                 nc.scalar.copy(y_rows[:, t0:t1, e * C : (e + 1) * C], turned[:])
-            for t in range((4, 4, 3, 4, 2, 2)[e]):
+            for t in (0, 1, 3, 2) if e < 4 else (0, 1):
                 scatter(t, e, e + 1, t == 3 and e >= 2)
 
         adapter_sum(0)
@@ -249,7 +249,7 @@ def tile_moe_elr_relu_kernel(
         gate_cols = held([P, E], F32, "gate_cols")
         nc.scalar.activation(gate_cols[:], gate_bank[:, 0:E], ACT.Copy)
         for e in range(E):
-            adapters = ((1,), (2, 3), (4,), (5,), (), ())[e]
+            adapters = ((1,), (2,), (3,), (4, 5), (), ())[e]
             for later in adapters:
                 adapter_sum(later)
             result_sum(e)
@@ -258,7 +258,6 @@ def tile_moe_elr_relu_kernel(
             result_turn(e)
         scatter(3, 4, E, True)
         scatter(2, 4, E, True)
-        scatter(3, 2, 3)
 
         out_rows = out_0.rearrange("(p t) c -> p t c", t=4)
         for t in (0, 3, 1, 2):

@@ -88,7 +88,8 @@ def tile_moe_elr_relu_kernel(
             src = wa_words[first : first + count].rearrange("e s p i d -> p (e s) (i d)")
             nc.sync.dma_start(tile[:].bitcast(I32), src.bitcast(I32))
             for e in range(count):
-                wa_t[first + e] = tile[:, PASSES * e : PASSES * (e + 1), :]
+                for s in range(PASSES):
+                    wa_t[first + e, s] = tile[:, PASSES * e + s, :]
 
         def load_w(first, count=1):
             tile = held([P, count * PASSES, 2 * N], U8, "w%d" % first)
@@ -109,12 +110,19 @@ def tile_moe_elr_relu_kernel(
         x_rows = x_scales.rearrange("s (q r) t -> r q s t", r=4)
         for r in range(4):
             nc.sync.dma_start(x_bytes[r:P:32, :, :].bitcast(I32), x_rows[r].bitcast(I32))
+        first_wa = [held([P, H], U32, "wa0_%d" % s) for s in range(PASSES)]
+
+        def load_first_wa(s):
+            nc.sync.dma_start(first_wa[s][:].bitcast(I32), wa_words[0, s].rearrange("p i d -> p (i d)").bitcast(I32))
+            wa_t[0, s] = first_wa[s][:]
+
+        load_first_wa(0)
         load_x(1)
-        load_wa(0)
         def load_wa_rows(pair):
             load_stacked(nc.sync, wa_rows[pair], wa_scales[2 * pair : 2 * pair + 2].rearrange("e s b i -> (e s) b i"))
 
         load_wa_rows(0)
+        load_first_wa(1)
         nc.sync.dma_start(gate_rows[:], gate.rearrange("r (e c) -> (r e) c", c=C)[0:P, :])
         load_w(0)
         load_wa(1)
@@ -186,7 +194,7 @@ def tile_moe_elr_relu_kernel(
             for s in range(PASSES):
                 nc.tensor.matmul_mx(
                     h_bank[:], lhsT=slot_words[e, s], lhsT_scale=slot_bytes[e, s],
-                    rhs=wa_t[e][:, s, :].bitcast(FP8X4), rhs_scale=wa_plane(e, s),
+                    rhs=wa_t[e, s].bitcast(FP8X4), rhs_scale=wa_plane(e, s),
                     start=(s == 0), stop=(s == PASSES - 1),
                 )
             h_pairs[e] = held([P, 2, P], F32, "h_pairs%d" % e)
@@ -242,7 +250,7 @@ def tile_moe_elr_relu_kernel(
 
         adapter_sum(0)
         adapter_turn(0)
-        gather_bytes(EARLY, 4, "wa0")
+        gather_bytes(EARLY, 4, "wa0_1")
         gather_bytes(4, E, "h_grouped0")
         gate_bank = bank([P, C], "gate_bank", 7)
         nc.tensor.transpose(gate_bank[:], gate_rows[:], identity[:])
@@ -296,8 +304,8 @@ def tile_moe_elr_relu_kernel(
                 out_words[:, columns].bitcast(FP8X4), out_plane[:, columns],
                 grouped[g][:].rearrange("p c u -> p (c u)").bitcast(BF16),
             )
-            if g % 2:
-                stored = slice((g - 1) * PIECE, (g + 1) * PIECE)
+            if g > 0:
+                stored = slice(0 if g == 1 else g * PIECE, (g + 1) * PIECE)
                 nc.sync.dma_start(words_dram[:, stored], out_words[:, stored].bitcast(I32))
         plane_dram = out_2[0].rearrange("(q r) t -> r q t", r=4)
         for r in range(4):

@@ -136,9 +136,9 @@ def tile_moe_elr_relu_kernel(
         load_side_by_side(nc.sync, w_rows[1], w_scales[2:4])
         load_wa(3)
         load_wb(2)
-        load_w(3)
         load_wa(4, 2)
         load_wa_rows(2)
+        load_w(3)
         load_wb(3)
         load_w(4, 2)
         load_side_by_side(nc.sync, w_rows[2], w_scales[4:6])
@@ -246,7 +246,7 @@ def tile_moe_elr_relu_kernel(
                     nc.tensor.transpose(turned[:, t - t0, :], y_dealt[e, t0][:, t - t0, :], identity[:])
                 nc.scalar.copy(y_rows[:, t0:t1, e * C : (e + 1) * C], turned[:])
             for t in (0, 1, 3, 2) if e < 4 else (0, 1):
-                scatter(t, e, e + 1, t == 3 and e >= 2)
+                scatter(t, e, e + 1, t == 3 and e % 2 == 1)
 
         adapter_sum(0)
         adapter_turn(0)

from contextlib import ExitStack

import concourse.mybir as mybir
from concourse.masks import make_identity

K, T, E, C, H, N = 1024, 1024, 6, 128, 512, 512
S = E * C
FLOPS = 2 * S * (K * H + K * N + H * N)

F32 = mybir.dt.float32
BF16 = mybir.dt.bfloat16
I32 = mybir.dt.int32
U32 = mybir.dt.uint32
U16 = mybir.dt.uint16
U8 = mybir.dt.uint8
FP8X4 = mybir.dt.float8_e4m3fn_x4
FP4X4 = mybir.dt.float4_e2m1fn_x4
ACT = mybir.ActivationFunctionType

P = 128
PASSES = K // 512
COLS = C // 16
EARLY = 2
PIECE = T // 4


def tile_moe_elr_relu_kernel(
    tc, x_words, x_scales, w_words, w_scales, wa_words, wa_scales, wb_words, wb_scales, gate, offs, out_0, out_1, out_2
):
    nc = tc.nc
    with ExitStack() as ctx:
        keep = ctx.enter_context(tc.tile_pool(name="keep", bufs=1))
        psum = ctx.enter_context(tc.psum_pool(name="psum", bufs=1))

        def held(shape, dtype, name, tag=None):
            return keep.tile(shape, dtype, name=name, tag=tag or name, align_bytes=64)

        def bank(shape, name, number):
            return psum.tile(shape, F32, name=name, tag="bank%d" % number)

        def zero(engine, tile):
            engine.memset(tile[:].bitcast(I32), 0)

        def load_side_by_side(queue, tile, scales):
            src = scales.rearrange("e s (q r) n -> r q (e s) n", r=4)
            for r in range(4):
                queue.dma_start(tile[r:P:32, :, :].bitcast(I32), src[r].bitcast(I32))

        def load_stacked(queue, tile, scales):
            count = scales.shape[0]
            for q in range(4):
                queue.dma_start(
                    tile[32 * q : 32 * q + 4 * count, :].bitcast(I32), scales[:, 4 * q : 4 * q + 4, :].bitcast(I32)
                )

        offsets = held([P, S // 16], U16, "offsets")
        x_table = held([P, PASSES * T], U32, "x_table")
        x_bytes = held([P, PASSES, T], U8, "x_bytes")
        wa_rows = [held([P, H], U8, "wa_rows%d" % pair) for pair in range(E // 2)]
        w_rows = [held([P, 2 * PASSES, N], U8, "w_rows%d" % pair) for pair in range(E // 2)]
        wb_first = held([P, N], U8, "wb_first")
        wb_last = held([P, N], U8, "wb_last")
        identity = held([P, P], F32, "identity")
        gate_rows = held([P, C], F32, "gate_rows")
        windows = [held([P, T], F32, "window%d" % t) for t in range(4)]

        zero(nc.gpsimd, w_rows[0])
        load_side_by_side(nc.gpsimd, w_rows[0], w_scales[0:2])
        make_identity(nc, identity[:])
        for tile in (x_bytes, wa_rows[0], wb_first, wa_rows[1], wa_rows[2]):
            zero(nc.vector, tile)
        zero(nc.gpsimd, w_rows[1])
        zero(nc.gpsimd, w_rows[2])
        for t in range(4):
            nc.gpsimd.memset(windows[t][:], 0.0)
        zero(nc.gpsimd, wb_last)
        load_stacked(nc.gpsimd, wb_last, wb_scales[4:E, 0])

        wa_t, w_t, wb_t = {}, {}, {}

        def load_x(s):
            nc.sync.dma_start(
                x_table[:, s * T : (s + 1) * T].bitcast(I32), x_words[s].rearrange("p t d -> p (t d)").bitcast(I32)
            )

        def load_wa(first, count=1):
            tile = held([P, count * PASSES, H], U32, "wa%d" % first)
            src = wa_words[first : first + count].rearrange("e s p i d -> p (e s) (i d)")
            nc.sync.dma_start(tile[:].bitcast(I32), src.bitcast(I32))
            for e in range(count):
                for s in range(PASSES):
                    wa_t[first + e, s] = tile[:, PASSES * e + s, :]

        def load_w(first, count=1):
            tile = held([P, count * PASSES, 2 * N], U8, "w%d" % first)
            src = w_words[first : first + count].rearrange("e s p b -> p (e s) b")
            nc.sync.dma_start(tile[:].bitcast(I32), src.bitcast(I32))
            for e in range(count):
                w_t[first + e] = tile[:, PASSES * e : PASSES * (e + 1), :]

        def load_wb(first, count=1):
            tile = held([P, count, N], U32, "wb%d" % first)
            src = wb_words[:, 0].rearrange("e p n d -> p e (n d)").bitcast(I32)
            nc.sync.dma_start(tile[:].bitcast(I32), src[:, first : first + count, :])
            for e in range(count):
                wb_t[first + e] = tile[:, e, :]

        nc.sync.dma_start(offsets[:], offs)
        load_x(0)
        x_rows = x_scales.rearrange("s (q r) t -> r q s t", r=4)
        for r in range(4):
            nc.sync.dma_start(x_bytes[r:P:32, :, :].bitcast(I32), x_rows[r].bitcast(I32))
        first_wa = [held([P, H], U32, "wa0_%d" % s) for s in range(PASSES)]

        def load_first_wa(s):
            nc.sync.dma_start(first_wa[s][:].bitcast(I32), wa_words[0, s].rearrange("p i d -> p (i d)").bitcast(I32))
            wa_t[0, s] = first_wa[s][:]

        load_first_wa(0)
        load_x(1)
        def load_wa_rows(pair):
            load_stacked(nc.sync, wa_rows[pair], wa_scales[2 * pair : 2 * pair + 2].rearrange("e s b i -> (e s) b i"))

        load_wa_rows(0)
        load_first_wa(1)
        nc.sync.dma_start(gate_rows[:], gate.rearrange("r (e c) -> (r e) c", c=C)[0:P, :])
        load_w(0)
        load_wa(1)
        load_wb(0)
        load_stacked(nc.sync, wb_first, wb_scales[0:4, 0])
        load_w(1)
        load_wa(2)
        load_wa_rows(1)
        load_wb(1)
        load_w(2)
        load_side_by_side(nc.sync, w_rows[1], w_scales[2:4])
        load_wa(3)
        load_wb(2)
        load_wa(4, 2)
        load_wa_rows(2)
        load_w(3)
        load_wb(3)
        load_w(4, 2)
        load_side_by_side(nc.sync, w_rows[2], w_scales[4:6])
        load_wb(4)
        load_wb(5)

        def wa_plane(e, s):
            return wa_rows[e // 2][4 * (PASSES * (e % 2) + s) : P, :]

        def w_plane(e, s):
            return w_rows[e // 2][:, PASSES * (e % 2) + s, :]

        def wb_plane(e):
            return (wb_first if e < 4 else wb_last)[4 * (e % 4) : P, :]

        slot_words, slot_bytes = {}, {}

        def gather_words(first, last):
            tile = held([P, PASSES, (last - first) * C], U32, "slot_words%d" % first)
            for s in range(PASSES):
                end = (s + 1) * T if first == 0 else PASSES * T
                nc.vector.tensor_copy(
                    tile[:, s, :], x_table[:, s * T : end].indirect(offsets[:, COLS * first : COLS * last])
                )
                for e in range(first, last):
                    slot_words[e, s] = tile[:, s, (e - first) * C : (e - first + 1) * C].bitcast(FP8X4)

        def gather_bytes(first, last, tag=None):
            tile = held([P, PASSES, (last - first) * C], U8, "slot_bytes%d" % first, tag)
            for s in range(PASSES):
                nc.vector.tensor_copy(tile[:, s, :], x_bytes[:, s, :].indirect(offsets[:, COLS * first : COLS * last]))
                for e in range(first, last):
                    slot_bytes[e, s] = tile[:, s, (e - first) * C : (e - first + 1) * C]

        gather_bytes(0, EARLY)
        gather_words(0, EARLY)
        gather_words(EARLY, E)

        y_rows = held([P, 4, S], F32, "y_rows")

        def scatter(t, first, last, on_scalar=False):
            target = windows[t][:].indirect(offsets[:, COLS * first : COLS * last])
            values = y_rows[:, t, first * C : last * C]
            if on_scalar:
                nc.scalar.activation(target, values, ACT.Copy)
            else:
                nc.vector.tensor_copy(target, values)

        h_pairs, hidden, y_dealt = {}, {}, {}

        def adapter_sum(e):
            h_bank = bank([P, H], "h_bank", (0, 0, 1, 0, 1, 0)[e])
            for s in range(PASSES):
                nc.tensor.matmul_mx(
                    h_bank[:], lhsT=slot_words[e, s], lhsT_scale=slot_bytes[e, s],
                    rhs=wa_t[e, s].bitcast(FP8X4), rhs_scale=wa_plane(e, s),
                    start=(s == 0), stop=(s == PASSES - 1),
                )
            h_pairs[e] = held([P, 2, P], F32, "h_pairs%d" % e)
            rounded = h_pairs[e][:].bitcast(BF16).rearrange("c u (p j) -> c u p j", j=2)
            sums = h_bank[:].rearrange("c (p u j) -> c u p j", u=2, j=2)
            for u0, u1 in ((0, 1), (1, 2)) if e == 0 else ((0, 2),):
                nc.scalar.activation(rounded[:, u0:u1], sums[:, u0:u1], ACT.Relu)

        def adapter_turn(e):
            turned = bank([P, 2, C], "h_turned", (4, 3, 2, 3, 2, 3)[e])
            for u in range(2):
                nc.tensor.transpose(turned[:, u, :], h_pairs[e][:, u, :], identity[:])
            h_grouped = held([P, C, 2], F32, "h_grouped%d" % e)
            nc.scalar.copy(h_grouped[:], turned[:].rearrange("p u c -> p c u"))
            h_words = held([P, C], U32, "h_words%d" % e)
            h_plane = held([P, C], U8, "h_plane%d" % e)
            nc.vector.quantize_mx(
                h_words[:].bitcast(FP8X4), h_plane[:], h_grouped[:].rearrange("p c u -> p (c u)").bitcast(BF16)
            )
            hidden[e] = (h_words, h_plane)

        def parts(e):
            return ((0, 1), (1, 4)) if e == 0 else ((0, 2), (2, 4))

        def result_sum(e):
            h_words, h_plane = hidden[e]
            y_bank = bank([P, N], "y_bank", (4, 5, 4, 5, 4, 1)[e])
            for s in range(PASSES):
                nc.tensor.matmul_mx(
                    y_bank[:], lhsT=slot_words[e, s], lhsT_scale=slot_bytes[e, s],
                    rhs=w_t[e][:, s, :].bitcast(FP4X4), rhs_scale=w_plane(e, s), start=(s == 0), stop=False,
                )
            nc.tensor.matmul_mx(
                y_bank[:], lhsT=h_words[:].bitcast(FP8X4), lhsT_scale=h_plane[:],
                rhs=wb_t[e].bitcast(FP8X4), rhs_scale=wb_plane(e), start=False, stop=True,
            )
            for t0, t1 in parts(e):
                y_dealt[e, t0] = held([P, t1 - t0, P], F32, "y_dealt%d_%d" % (e, t0))
                nc.scalar.activation(
                    y_dealt[e, t0][:], y_bank[:].rearrange("c (p t) -> c t p", t=4)[:, t0:t1, :], ACT.Copy,
                    scale=gate_cols[:, e : e + 1],
                )

        def result_turn(e):
            for t0, t1 in parts(e):
                number = (6 if e < 5 else 2) + (t0 > 0)
                turned = bank([P, t1 - t0, C], "y_turned", number)
                for t in range(t0, t1):
                    nc.tensor.transpose(turned[:, t - t0, :], y_dealt[e, t0][:, t - t0, :], identity[:])
                nc.scalar.copy(y_rows[:, t0:t1, e * C : (e + 1) * C], turned[:])
            for t in (0, 1, 3, 2) if e < 4 else (0, 1):
                scatter(t, e, e + 1, t == 3 and e % 2 == 1)

        adapter_sum(0)
        adapter_turn(0)
        gather_bytes(EARLY, 4, "wa0_1")
        gather_bytes(4, E, "h_grouped0")
        gate_bank = bank([P, C], "gate_bank", 7)
        nc.tensor.transpose(gate_bank[:], gate_rows[:], identity[:])
        gate_cols = held([P, E], F32, "gate_cols")
        nc.scalar.activation(gate_cols[:], gate_bank[:, 0:E], ACT.Copy)
        for e in range(E):
            adapters = ((1,), (2,), (3,), (4, 5), (), ())[e]
            for later in adapters:
                adapter_sum(later)
            result_sum(e)
            for later in adapters:
                adapter_turn(later)
            result_turn(e)
        scatter(3, 4, E, True)
        scatter(2, 4, E, True)

        out_rows = out_0.rearrange("(p t) c -> p t c", t=4)
        for t in (0, 3, 1, 2):
            nc.sync.dma_start(out_rows[:, t, :], windows[t][:])

        pairs = [held([P, 2, PIECE], F32, "pairs%d" % g) for g in range(4)]

        def round_rows(t, g, on_scalar=False):
            u, j = divmod(t, 2)
            target = pairs[g][:, u, :].bitcast(BF16).rearrange("p (c j) -> p c j", j=2)[:, :, j]
            values = windows[t][:, g * PIECE : (g + 1) * PIECE]
            if on_scalar:
                nc.scalar.copy(target, values)
            else:
                nc.vector.tensor_copy(target, values)

        for t in (0, 1):
            for g in (2, 3, 0, 1):
                round_rows(t, g)
        for t in (3, 2):
            for g in range(4):
                round_rows(t, g, g >= 2)

        out_words = held([P, T], U32, "out_words")
        out_plane = held([P, T], U8, "out_plane")
        words_dram = out_1[0].rearrange("p t d -> p (t d)").bitcast(I32)
        grouped = [held([P, PIECE, 2], F32, "grouped%d" % g) for g in range(4)]
        for g in range(4):
            if g < 2:
                nc.vector.tensor_copy(grouped[g][:].bitcast(I32), pairs[g][:].bitcast(I32).rearrange("p u c -> p c u"))
            else:
                nc.scalar.copy(grouped[g][:], pairs[g][:].rearrange("p u c -> p c u"))
        for g in range(4):
            columns = slice(g * PIECE, (g + 1) * PIECE)
            nc.vector.quantize_mx(
                out_words[:, columns].bitcast(FP8X4), out_plane[:, columns],
                grouped[g][:].rearrange("p c u -> p (c u)").bitcast(BF16),
            )
            if g > 0:
                stored = slice(0 if g == 1 else g * PIECE, (g + 1) * PIECE)
                nc.sync.dma_start(words_dram[:, stored], out_words[:, stored].bitcast(I32))
        plane_dram = out_2[0].rearrange("(q r) t -> r q t", r=4)
        for r in range(4):
            (nc.sync, nc.scalar)[r % 2].dma_start(plane_dram[r].bitcast(I32), out_plane[r:P:32, :].bitcast(I32))
